import numpy as np
import ml_dtypes


def mxq(x, axis, fmt="e4m3"):
    dtype, down = {"e4m3": (ml_dtypes.float8_e4m3fn, 7), "e5m2": (ml_dtypes.float8_e5m2, 14)}[fmt]
    v = np.moveaxis(np.asarray(x, np.float32).astype(ml_dtypes.bfloat16).astype(np.float64), axis, -1)
    blocks = v.reshape(v.shape[:-1] + (-1, 32))
    amax = np.abs(blocks).max(-1, keepdims=True)
    byte = np.maximum(np.where(amax > 0, np.frexp(amax)[1] - 1 + 127, 0) - down, 1)
    scale = np.exp2(byte - 127.0)
    codes = (blocks / scale).astype(np.float32).astype(dtype).astype(np.float64)
    return np.moveaxis((codes * scale).reshape(v.shape), -1, axis)


WIDE = False


def mx_kscale(k):
    if not WIDE:
        return np.ones(k)
    levels = np.array([10, -10, 5, -5, 0])
    if k % 512:
        return np.exp2(np.random.permutation(np.resize(levels, k // 32))).repeat(32)
    a = np.empty((k // 512, 16))
    for p in range(k // 512):
        a[p, :8] = np.random.permutation(np.resize(levels, 8))
        for g in range(8):
            far = levels[np.abs(levels - a[p, g]) >= 10]
            a[p, g + 8] = far[np.random.randint(len(far))]
    return np.exp2(a.ravel()).repeat(32)


def f64(x):
    return np.asarray(x).astype(np.float64)


def striped(idx):
    return np.tile(idx.reshape(-1, 16).T, (8, 1)).astype(np.uint16)


def unstriped(offs):
    return offs[:16].T.reshape(-1).astype(np.int64)


E2M1 = np.array([0.0, 0.5, 1.0, 1.5, 2.0, 3.0, 4.0, 6.0, -0.0, -0.5, -1.0, -1.5, -2.0, -3.0, -4.0, -6.0])


def pack_weight(w, fmt):
    k, n = w.shape
    w = f64(np.asarray(w, np.float32).astype(ml_dtypes.bfloat16)).reshape(k // 32, 32, n)
    amax = np.abs(w).max(1)
    if fmt == "e4m3":
        byte = np.frexp(amax)[1] - 1 + 127 - 7
    else:
        mant, ex = np.frexp(amax / 6.0)
        byte = np.where(mant > 0.5, ex, ex - 1) + 127
    byte = np.clip(np.where(amax > 0, byte, 1), 1, 254)
    scaled = (w * np.exp2(127.0 - byte)[:, None, :]).reshape(k, n).astype(np.float32)
    by_word = np.ascontiguousarray(scaled.reshape(k // 512, 128, 4, n).transpose(0, 1, 3, 2))
    if fmt == "e4m3":
        words = by_word.astype(ml_dtypes.float8_e4m3fn).view(np.uint8)
    else:
        c = by_word.astype(ml_dtypes.float4_e2m1fn).view(np.uint8) & 0xF
        words = (c[..., 0::2] | (c[..., 1::2] << 4)).reshape(k // 512, 128, 2 * n)
    return np.ascontiguousarray(words), np.ascontiguousarray(byte.astype(np.uint8).reshape(k // 512, 16, n))


def unpack_weight(words, scales, fmt):
    g, _, n = scales.shape
    words = np.ascontiguousarray(words).reshape(g, 128, n, -1)
    if fmt == "e4m3":
        vals = words.view(ml_dtypes.float8_e4m3fn).astype(np.float64)
    else:
        nib = np.empty((g, 128, n, 4), np.uint8)
        nib[..., 0::2] = words & 0xF
        nib[..., 1::2] = words >> 4
        vals = E2M1[nib]
    vals = vals * np.repeat(np.exp2(scales.astype(np.float64) - 127.0), 8, axis=1)[..., None]
    return vals.transpose(0, 1, 3, 2).reshape(g * 512, n)


def gelu(v):
    return 0.5 * v * (1.0 + np.tanh(np.sqrt(2.0 / np.pi) * (v + 0.044715 * v**3)))


K, K2, H, N, T, S = 512, 1024, 1024, 384, 4096, 1024

def setup_inputs():
    n = np.random.standard_normal
    s = mx_kscale(K)[:, None]
    s2 = mx_kscale(K2)[:, None]
    u = mx_kscale(H)[:, None]
    d = {}
    d["tab_words"], d["tab_scales"] = pack_weight(n((K, T)) * s, "e4m3")
    d["offs"] = striped(np.random.permutation(T)[:S])
    d["xs_words"], d["xs_scales"] = pack_weight(n((K2, S)) * s2, "e4m3")
    d["wa"] = (n((K, H)) / K ** 0.5 / s * u.T).astype(np.float32)
    d["wb_words"], d["wb_scales"] = pack_weight(n((K, H)) / K ** 0.5 / s * u.T, "e2m1")
    d["ws"] = (n((K2, H)) / K2 ** 0.5 / s2 * u.T).astype(np.float32)
    d["wo"] = (1.3 * n((H, N)) / H ** 0.5 / u).astype(np.float32)
    d["bo"] = (0.6 * n(N)).astype(np.float32)
    return d

def reference(tab_words, tab_scales, offs, xs_words, xs_scales, wa, wb_words, wb_scales, ws, wo, bo):
    v = unpack_weight(tab_words, tab_scales, "e4m3")[:, unstriped(offs)]
    xs = unpack_weight(xs_words, xs_scales, "e4m3")
    wb = unpack_weight(wb_words, wb_scales, "e2m1")
    a = mxq(f64(wa), 0, "e4m3").T @ v
    b = wb.T @ v
    e = mxq(f64(ws), 0, "e4m3").T @ xs
    h = np.abs(a - e) - np.abs(b - e)
    y = mxq(f64(wo), 0, "e4m3").T @ mxq(h, 0, "e4m3")
    return np.tanh(y + f64(bo)[:, None])

@@ -1,0 +1,332 @@
+from contextlib import ExitStack
+
+import concourse.mybir as mybir
+
+K, K2, H, N, T, S = 512, 1024, 1024, 384, 4096, 1024
+FLOPS = 2 * S * (2 * K * H + K2 * H + H * N)
+
+F32 = mybir.dt.float32
+BF16 = mybir.dt.bfloat16
+I32 = mybir.dt.int32
+U32 = mybir.dt.uint32
+U16 = mybir.dt.uint16
+U8 = mybir.dt.uint8
+FP8X4 = mybir.dt.float8_e4m3fn_x4
+FP4X4 = mybir.dt.float4_e2m1fn_x4
+ALU = mybir.AluOpType
+ACT = mybir.ActivationFunctionType
+
+P = 128
+PACK = 4
+PASS = P * PACK
+GROUPS = H // PASS
+COLS = 128
+STRIPS = S // COLS
+HALF = 512
+OUT_TILES = N // P
+CHUNKS = ((0, 512), (512, 256), (768, 128), (896, 128))
+TWICE = ((0, 5), (1, 3), (1, 6), )
+SUB_ON_VECTOR = ((0, 0), (0, 1), (0, 2), (0, 3), (0, 4), (0, 5), (0, 6), (0, 7), (1, 0), (1, 1), (1, 2), (1, 3), (1, 4), (1, 5), (1, 6), (1, 7), )
+COPY_ON_VECTOR = ()
+LATE_CASTS = (("scalar", "scalar", "vector", "vector"), ("scalar", "scalar", "vector", "vector"), ("scalar", "scalar", "vector", "vector"), ("scalar", "scalar", "vector", "vector"))
+
+
+def tile_list_typewriter_strokes_kernel(
+    tc, tab_words, tab_scales, offs, xs_words, xs_scales, wa, wb_words, wb_scales, ws, wo, bo, out
+):
+    nc = tc.nc
+    with ExitStack() as ctx:
+        keep = ctx.enter_context(tc.tile_pool(name="keep", bufs=1))
+        ring = ctx.enter_context(tc.tile_pool(name="ring", bufs=3))
+        psum = ctx.enter_context(tc.psum_pool(name="psum", bufs=2))
+
+        offsets = keep.tile([P, S // 16], U16, name="offsets")
+        xs_plane = keep.tile([P, S], U8, name="xs_plane", align_bytes=64)
+        wb_plane_raw = keep.tile([P, H], U8, name="wb_plane_raw", align_bytes=64)
+        tab_plane = keep.tile([P, T], U8, name="tab_plane", align_bytes=64)
+        nc.gpsimd.memset(tab_plane[:].bitcast(I32), 0)
+        nc.vector.memset(xs_plane[:].bitcast(I32), 0)
+        nc.vector.memset(wb_plane_raw[:].bitcast(I32), 0)
+
+        def load_rows(name, w, k0, c0):
+            raw = keep.tile([P, PACK, PASS], F32, name=name)
+            nc.sync.dma_start(
+                out=raw[:], in_=w[k0 : k0 + PASS, c0 : c0 + PASS].rearrange("(p j) c -> p j c", j=PACK)
+            )
+            return raw
+
+        def load_xs(jh):
+            words = keep.tile([P, 2, HALF], I32, name="xs_codes%d" % jh, align_bytes=64)
+            src = xs_words.rearrange("a p c i -> p a (c i)")[:, :, 4 * HALF * jh : 4 * HALF * (jh + 1)]
+            nc.sync.dma_start(out=words[:], in_=src.bitcast(I32))
+            return words
+
+        def load_plane(plane, rows, depth):
+            for q in range(4):
+                nc.sync.dma_start(
+                    out=plane[32 * q : 32 * q + 4 * depth, :].bitcast(I32),
+                    in_=rows[:, 4 * q : 4 * q + 4, :].bitcast(I32),
+                )
+
+        xs_codes = {}
+        ws_raw = {}
+        wa_raw = {}
+        nc.sync.dma_start(offsets[:], offs)
+        ws_raw[0, 0] = load_rows("ws_raw00", ws, 0, 0)
+        xs_codes[0] = load_xs(0)
+        ws_raw[0, 1] = load_rows("ws_raw01", ws, PASS, 0)
+        load_plane(xs_plane, xs_scales, 2)
+        load_plane(tab_plane, tab_scales, 1)
+        wb_raw = keep.tile([P, 2 * H], U8, name="wb_raw", align_bytes=64)
+        nc.sync.dma_start(out=wb_raw[:].bitcast(I32), in_=wb_words[0].bitcast(I32))
+        load_plane(wb_plane_raw, wb_scales, 1)
+        tab = keep.tile([P, T], I32, name="tab", align_bytes=64)
+        nc.sync.dma_start(out=tab[:], in_=tab_words[0].rearrange("p t i -> p (t i)").bitcast(I32))
+        wa_raw[0] = load_rows("wa_raw0", wa, 0, 0)
+        xs_codes[1] = load_xs(1)
+        ws_raw[1, 0] = load_rows("ws_raw10", ws, 0, PASS)
+        ws_raw[1, 1] = load_rows("ws_raw11", ws, PASS, PASS)
+        wa_raw[1] = load_rows("wa_raw1", wa, 0, PASS)
+        wo_raw = {}
+        wo_rows = wo.rearrange("(b g t i) n -> b t g i n", b=GROUPS, g=16, t=PACK)
+        for b in range(GROUPS):
+            wo_raw[b] = keep.tile([P, PACK, N], F32, name="wo_raw%d" % b)
+            for t in range(PACK):
+                nc.sync.dma_start(out=wo_raw[b][:, t, :], in_=wo_rows[b, t])
+        bias = keep.tile([P, OUT_TILES], F32, name="bias")
+        with nc.allow_non_contiguous_dma(reason="one bias value a partition"):
+            nc.sync.dma_start(out=bias[:], in_=bo.rearrange("(c p) -> p c", p=P))
+
+        def scale_cast(engine, dst, src, factor):
+            if engine == "vector":
+                nc.vector.tensor_scalar(out=dst, in0=src, scalar1=factor, scalar2=None, op0=ALU.mult)
+            elif engine == "scalar":
+                nc.scalar.activation(out=dst, in_=src, func=ACT.Copy, scale=factor)
+            else:
+                nc.gpsimd.tensor_scalar(
+                    out=dst, in0=src, scalar1=factor, scalar2=0.0, op0=ALU.mult, op1=ALU.add
+                )
+
+        def round_weight(name, raw, factor, engines):
+            grouped = keep.tile([P, PACK, PASS], BF16, name=name, align_bytes=64)
+            src = raw[:].rearrange("p j (g t i) -> p t g i j", t=PACK, i=8)
+            dst = grouped[:].rearrange("p t (g i j) -> p t g i j", i=8, j=PACK)
+            for t in range(PACK):
+                scale_cast(engines[t], dst[:, t], src[:, t], factor)
+            return grouped
+
+        def quantize(name, grouped, width):
+            codes = keep.tile([P, width], U32, name=name + "_codes", align_bytes=64)
+            scales = keep.tile([P, width], U8, name=name + "_scales", align_bytes=64)
+            nc.vector.quantize_mx(out=codes[:].bitcast(FP8X4), scales=scales[:], in_=grouped)
+            return codes, scales
+
+        def weight(name, raw, factor, engines):
+            grouped = round_weight(name + "_bf", raw, factor, engines)
+            return quantize(name, grouped[:].rearrange("p t c -> p (t c)"), PASS)
+
+        ws_q = {}
+        wa_q = {}
+        v_codes = {}
+        v_scales = {}
+        head = ("vector", "vector", "scalar", "vector")
+        head_a = ("scalar", "scalar", "gpsimd", "gpsimd")
+
+        def gather_scales(jh):
+            v_scales[jh] = keep.tile([P, HALF], U8, name="v_scales%d" % jh, align_bytes=64)
+            nc.vector.tensor_copy(v_scales[jh][:], tab_plane[:].indirect(offsets[:, 32 * jh : 32 * (jh + 1)]))
+
+        def gather_codes(jh):
+            v_codes[jh] = keep.tile([P, HALF], U32, name="v_codes%d" % jh, tag="half%d" % jh, align_bytes=64)
+            nc.vector.tensor_copy(
+                v_codes[jh][:], tab[:].bitcast(U32).indirect(offsets[:, 32 * jh : 32 * (jh + 1)])
+            )
+
+        def e_passes(bank, b, q, t, start, stop):
+            jh, c0 = divmod(q * COLS, HALF)
+            for a in range(2):
+                codes, scales = ws_q[b, a]
+                nc.tensor.matmul_mx(
+                    out=bank[:, t, :],
+                    lhsT=codes[:, t * P : (t + 1) * P].bitcast(FP8X4),
+                    lhsT_scale=scales[:, t * P : (t + 1) * P],
+                    rhs=xs_codes[jh][:, a, c0 : c0 + COLS].bitcast(FP8X4),
+                    rhs_scale=xs_plane[4 * a :, q * COLS : (q + 1) * COLS],
+                    start=start and a == 0,
+                    stop=stop and a == 1,
+                )
+
+        def v_pass(bank, lhsT, lhsT_scale, q, t, stop):
+            jh, c0 = divmod(q * COLS, HALF)
+            nc.tensor.matmul_mx(
+                out=bank[:, t, :],
+                lhsT=lhsT,
+                lhsT_scale=lhsT_scale,
+                rhs=v_codes[jh][:, c0 : c0 + COLS].bitcast(FP8X4),
+                rhs_scale=v_scales[jh][:, c0 : c0 + COLS],
+                start=True,
+                stop=stop,
+            )
+
+        def woven(bank):
+            return bank[:].rearrange("p t n -> p n t")
+
+        neg_e = {}
+        dist = {}
+        h_bf = {}
+        h_q = {}
+
+        def stage_e(b, q):
+            if (b, q) in TWICE:
+                return
+            bank = psum.tile([P, PACK, COLS], F32, name="bank_e")
+            for t in range(PACK):
+                e_passes(bank, b, q, t, True, True)
+            neg_e[b, q] = ring.tile([P, COLS, PACK], F32, name="neg_e", bufs=6)
+            if (b, q) in COPY_ON_VECTOR:
+                nc.vector.tensor_copy(out=neg_e[b, q][:], in_=woven(bank))
+            else:
+                nc.scalar.copy(out=neg_e[b, q][:], in_=woven(bank))
+
+        def distance(b, q, side):
+            twice = (b, q) in TWICE
+            bank = psum.tile([P, PACK, COLS], F32, name="bank_" + side)
+            for t in range(PACK):
+                if side == "a":
+                    codes, scales = wa_q[b]
+                    lhsT = codes[:, t * P : (t + 1) * P].bitcast(FP8X4)
+                    lhsT_scale = scales[:, t * P : (t + 1) * P]
+                else:
+                    c0 = b * PASS + t * P
+                    lhsT = wb_codes[:, 2 * c0 : 2 * (c0 + P)].bitcast(FP4X4)
+                    lhsT_scale = wb_plane[:, c0 : c0 + P]
+                v_pass(bank, lhsT, lhsT_scale, q, t, not twice)
+                if twice:
+                    e_passes(bank, b, q, t, False, True)
+            dist[b, q, side] = ring.tile([P, COLS, PACK], F32, name="dist_" + side, bufs=5)
+            if twice:
+                nc.scalar.activation(out=dist[b, q, side][:], in_=woven(bank), func=ACT.Abs)
+            else:
+                if (b, q, side) == (0, 0, "b"):
+                    diff = keep.tile([P, COLS, PACK], F32, name="diff_first", tag="half1", align_bytes=64)
+                else:
+                    diff = ring.tile([P, COLS, PACK], F32, name="diff_" + side)
+                nc.vector.tensor_tensor(out=diff[:], in0=woven(bank), in1=neg_e[b, q][:], op=ALU.add)
+                nc.scalar.activation(
+                    out=dist[b, q, side][:].rearrange("p n t -> p (n t)"),
+                    in_=diff[:].rearrange("p n t -> p (n t)"),
+                    func=ACT.Abs,
+                )
+
+        def h_piece(b, q):
+            pieces = CHUNKS if b == GROUPS - 1 else ((0, HALF), (HALF, HALF))
+            for j0, width in pieces:
+                if j0 <= q * COLS < j0 + width:
+                    return j0, width
+
+        def stage_h(b, q):
+            j0, width = h_piece(b, q)
+            if q * COLS == j0:
+                h_bf[b, j0] = keep.tile([P, PACK * width], BF16, name="h_bf%d_%d" % (b, j0), align_bytes=64)
+            e0 = PACK * (q * COLS - j0)
+            engine = nc.vector if (b, q) in SUB_ON_VECTOR else nc.gpsimd
+            engine.tensor_tensor(
+                out=h_bf[b, j0][:, e0 : e0 + PASS],
+                in0=dist[b, q, "a"][:].rearrange("p n t -> p (n t)"),
+                in1=dist[b, q, "b"][:].rearrange("p n t -> p (n t)"),
+                op=ALU.subtract,
+            )
+
+        def stage_quant(b, q):
+            j0, width = h_piece(b, q)
+            if (q + 1) * COLS == j0 + width:
+                h_q[b, j0] = quantize("h%d_%d" % (b, j0), h_bf[b, j0][:], width)
+
+        def stage_out(q):
+            j0, width = h_piece(GROUPS - 1, q)
+            if (q + 1) * COLS != j0 + width:
+                return
+            result = keep.tile([P, OUT_TILES, width], F32, name="result%d" % j0)
+            for c in range(OUT_TILES):
+                bank = psum.tile([P, HALF], F32, name="bank_y")
+                for b in range(GROUPS):
+                    p0 = h_piece(b, q)[0]
+                    codes, scales = h_q[b, p0]
+                    cols = slice(j0 - p0, j0 - p0 + width)
+                    w0 = b * N + c * P
+                    nc.tensor.matmul_mx(
+                        out=bank[:, 0:width],
+                        lhsT=wo_codes[:, w0 : w0 + P].bitcast(FP8X4),
+                        lhsT_scale=wo_scales[:, w0 : w0 + P],
+                        rhs=codes[:, cols].bitcast(FP8X4),
+                        rhs_scale=scales[:, cols],
+                        start=b == 0,
+                        stop=b == GROUPS - 1,
+                    )
+                nc.scalar.activation(
+                    out=result[:, c, :], in_=bank[:, 0:width], func=ACT.Tanh, bias=bias[:, c : c + 1]
+                )
+            nc.sync.dma_start(
+                out=out[:, j0 : j0 + width].rearrange("(c p) j -> p c j", p=P), in_=result[:]
+            )
+
+        ws_q[0, 0] = weight("ws00", ws_raw[0, 0], -1.0, head)
+        ws_q[0, 1] = weight("ws01", ws_raw[0, 1], -1.0, head)
+        for q in range(4):
+            stage_e(0, q)
+        gather_scales(0)
+        wb_codes = keep.tile([P, 2 * H], U8, name="wb_codes", align_bytes=64)
+        wb_plane = keep.tile([P, H], U8, name="wb_plane", align_bytes=64)
+        for dst, src, words in ((wb_codes, wb_raw, 4), (wb_plane, wb_plane_raw, 2)):
+            nc.vector.tensor_copy(
+                out=dst[:].bitcast(I32).rearrange("p (b t g w) -> p b t g w", b=GROUPS, t=PACK, w=words),
+                in_=src[:].bitcast(I32).rearrange("p (b g t w) -> p b t g w", b=GROUPS, t=PACK, w=words),
+            )
+        gather_scales(1)
+        gather_codes(0)
+        wa_q[0] = weight("wa0", wa_raw[0], 1.0, head_a)
+        for q in range(4):
+            distance(0, q, "b")
+        gather_codes(1)
+
+        wo_bf = keep.tile([P, GROUPS, N, PACK], BF16, name="wo_bf", align_bytes=64)
+        wo_codes = keep.tile([P, GROUPS * N], U32, name="wo_codes", align_bytes=64)
+        wo_scales = keep.tile([P, GROUPS * N], U8, name="wo_scales", align_bytes=64)
+
+        steps = [(b, q) for b in range(GROUPS) for q in range(STRIPS)]
+        for k in range(len(steps) + 2):
+            if k >= 2:
+                stage_quant(*steps[k - 2])
+                if steps[k - 2][0] == GROUPS - 1:
+                    stage_out(steps[k - 2][1])
+            if 4 <= k + 2 < len(steps):
+                stage_e(*steps[k + 2])
+            if k < len(steps):
+                distance(*steps[k], "a")
+                if k >= 4:
+                    distance(*steps[k], "b")
+            if 1 <= k <= len(steps):
+                stage_h(*steps[k - 1])
+            if k == 2:
+                ws_q[1, 0] = weight("ws10", ws_raw[1, 0], -1.0, LATE_CASTS[0])
+            if k == 3:
+                ws_q[1, 1] = weight("ws11", ws_raw[1, 1], -1.0, LATE_CASTS[1])
+            if k == 5:
+                wa_q[1] = weight("wa1", wa_raw[1], 1.0, LATE_CASTS[2])
+            if k == 8:
+                for b in range(GROUPS):
+                    for u in range(2):
+                        cols = slice(u * N // 2, (u + 1) * N // 2)
+                        scale_cast(
+                            LATE_CASTS[3][2 * b + u],
+                            wo_bf[:, b, cols, :],
+                            wo_raw[b][:].rearrange("p t n -> p n t")[:, cols, :],
+                            1.0,
+                        )
+                flat = wo_bf[:].rearrange("p b n t -> p (b n t)")
+                for w0, w1 in ((0, 512), (512, 768)):
+                    nc.vector.quantize_mx(
+                        out=wo_codes[:, w0:w1].bitcast(FP8X4),
+                        scales=wo_scales[:, w0:w1],
+                        in_=flat[:, PACK * w0 : PACK * w1],
+                    )

@@ -19,16 +19,20 @@ ACT = mybir.ActivationFunctionType
 P = 128
 PACK = 4
 PASS = P * PACK
+BLOCKS = 16
+RUN = 8
 GROUPS = H // PASS
 COLS = 128
 STRIPS = S // COLS
 HALF = 512
 OUT_TILES = N // P
-CHUNKS = ((0, 512), (512, 256), (768, 128), (896, 128))
-TWICE = ((0, 5), (1, 3), (1, 6), )
+EARLY = 4
+CHUNKS = (((0, 512), (512, 512)), ((0, 512), (512, 256), (768, 128), (896, 128)))
+STEPS = ((0, 0), (0, 1), (0, 2), (0, 3), (0, 4), (0, 5), (0, 6), (0, 7), (1, 0), (1, 1), (1, 2), (1, 3), (1, 4), (1, 5), (1, 6), (1, 7), )
+TWICE = ((1, 1), (1, 4), (1, 7), )
 SUB_ON_VECTOR = ((0, 0), (0, 1), (0, 2), (0, 3), (0, 4), (0, 5), (0, 6), (0, 7), (1, 0), (1, 1), (1, 2), (1, 3), (1, 4), (1, 5), (1, 6), (1, 7), )
 COPY_ON_VECTOR = ()
-LATE_CASTS = (("scalar", "scalar", "vector", "vector"), ("scalar", "scalar", "vector", "vector"), ("scalar", "scalar", "vector", "vector"), ("scalar", "scalar", "vector", "vector"))
+SHARES = {"ws00": (("vector", 0, 12), ("scalar", 12, 16), ), "ws01": (("vector", 0, 12), ("scalar", 12, 16), ), "wa0": (("scalar", 0, 8), ("gpsimd", 8, 16), ), "ws10": (("gpsimd", 0, 16), ), "ws11": (("gpsimd", 0, 16), ), "wa1": (("scalar", 0, 16), ), "wo0": (("scalar", 0, 16), ), "wo1": (("vector", 0, 16), )}
 
 
 def tile_list_typewriter_strokes_kernel(
@@ -47,9 +51,12 @@ def tile_list_typewriter_strokes_kernel(
         nc.gpsimd.memset(tab_plane[:].bitcast(I32), 0)
         nc.vector.memset(xs_plane[:].bitcast(I32), 0)
         nc.vector.memset(wb_plane_raw[:].bitcast(I32), 0)
+        warm = keep.tile([P, 2], F32, name="warm")
+        nc.vector.memset(warm[:, 0:1], 0.0)
+        nc.scalar.activation(out=warm[:, 1:2], in_=warm[:, 0:1], func=ACT.Tanh)
 
-        def load_rows(name, w, k0, c0):
-            raw = keep.tile([P, PACK, PASS], F32, name=name)
+        def load_rows(w, k0, c0):
+            raw = ring.tile([P, PACK, PASS], F32, name="raw", bufs=4)
             nc.sync.dma_start(
                 out=raw[:], in_=w[k0 : k0 + PASS, c0 : c0 + PASS].rearrange("(p j) c -> p j c", j=PACK)
             )
@@ -68,34 +75,12 @@ def tile_list_typewriter_strokes_kernel(
                     in_=rows[:, 4 * q : 4 * q + 4, :].bitcast(I32),
                 )
 
-        xs_codes = {}
-        ws_raw = {}
-        wa_raw = {}
-        nc.sync.dma_start(offsets[:], offs)
-        ws_raw[0, 0] = load_rows("ws_raw00", ws, 0, 0)
-        xs_codes[0] = load_xs(0)
-        ws_raw[0, 1] = load_rows("ws_raw01", ws, PASS, 0)
-        load_plane(xs_plane, xs_scales, 2)
-        load_plane(tab_plane, tab_scales, 1)
-        wb_raw = keep.tile([P, 2 * H], U8, name="wb_raw", align_bytes=64)
-        nc.sync.dma_start(out=wb_raw[:].bitcast(I32), in_=wb_words[0].bitcast(I32))
-        load_plane(wb_plane_raw, wb_scales, 1)
-        tab = keep.tile([P, T], I32, name="tab", align_bytes=64)
-        nc.sync.dma_start(out=tab[:], in_=tab_words[0].rearrange("p t i -> p (t i)").bitcast(I32))
-        wa_raw[0] = load_rows("wa_raw0", wa, 0, 0)
-        xs_codes[1] = load_xs(1)
-        ws_raw[1, 0] = load_rows("ws_raw10", ws, 0, PASS)
-        ws_raw[1, 1] = load_rows("ws_raw11", ws, PASS, PASS)
-        wa_raw[1] = load_rows("wa_raw1", wa, 0, PASS)
-        wo_raw = {}
-        wo_rows = wo.rearrange("(b g t i) n -> b t g i n", b=GROUPS, g=16, t=PACK)
-        for b in range(GROUPS):
-            wo_raw[b] = keep.tile([P, PACK, N], F32, name="wo_raw%d" % b)
+        def load_wo(b):
+            raw = ring.tile([P, PACK, N], F32, name="raw", bufs=4)
+            rows = wo.rearrange("(b g t i) n -> b t g i n", b=GROUPS, g=BLOCKS, t=PACK)
             for t in range(PACK):
-                nc.sync.dma_start(out=wo_raw[b][:, t, :], in_=wo_rows[b, t])
-        bias = keep.tile([P, OUT_TILES], F32, name="bias")
-        with nc.allow_non_contiguous_dma(reason="one bias value a partition"):
-            nc.sync.dma_start(out=bias[:], in_=bo.rearrange("(c p) -> p c", p=P))
+                nc.sync.dma_start(out=raw[:, t, :], in_=rows[b, t])
+            return raw
 
         def scale_cast(engine, dst, src, factor):
             if engine == "vector":
@@ -107,71 +92,67 @@ def tile_list_typewriter_strokes_kernel(
                     out=dst, in0=src, scalar1=factor, scalar2=0.0, op0=ALU.mult, op1=ALU.add
                 )
 
-        def round_weight(name, raw, factor, engines):
-            grouped = keep.tile([P, PACK, PASS], BF16, name=name, align_bytes=64)
-            src = raw[:].rearrange("p j (g t i) -> p t g i j", t=PACK, i=8)
-            dst = grouped[:].rearrange("p t (g i j) -> p t g i j", i=8, j=PACK)
-            for t in range(PACK):
-                scale_cast(engines[t], dst[:, t], src[:, t], factor)
-            return grouped
+        def round_weight(name, grouped, raw, factor):
+            src = raw[:].rearrange("p j (g t i) -> p g t i j", t=PACK, i=RUN)
+            dst = grouped.rearrange("p (t g i j) -> p g t i j", t=PACK, i=RUN, j=PACK)
+            for engine, g0, g1 in SHARES[name]:
+                scale_cast(engine, dst[:, g0:g1], src[:, g0:g1], factor)
 
-        def quantize(name, grouped, width):
+        def round_wo(name, grouped, raw):
+            src = raw[:].rearrange("p t (g n) -> p g n t", g=BLOCKS)
+            dst = grouped.rearrange("p (g n t) -> p g n t", g=BLOCKS, t=PACK)
+            for engine, g0, g1 in SHARES[name]:
+                scale_cast(engine, dst[:, g0:g1], src[:, g0:g1], 1.0)
+
+        def quantize(name, grouped):
+            width = grouped.shape[1] // PACK
             codes = keep.tile([P, width], U32, name=name + "_codes", align_bytes=64)
             scales = keep.tile([P, width], U8, name=name + "_scales", align_bytes=64)
             nc.vector.quantize_mx(out=codes[:].bitcast(FP8X4), scales=scales[:], in_=grouped)
             return codes, scales
 
-        def weight(name, raw, factor, engines):
-            grouped = round_weight(name + "_bf", raw, factor, engines)
-            return quantize(name, grouped[:].rearrange("p t c -> p (t c)"), PASS)
+        def columns(operand, c0, width):
+            codes, scales = operand
+            return codes[:, c0 : c0 + width].bitcast(FP8X4), scales[:, c0 : c0 + width]
 
         ws_q = {}
         wa_q = {}
+        wo_q = {}
         v_codes = {}
         v_scales = {}
-        head = ("vector", "vector", "scalar", "vector")
-        head_a = ("scalar", "scalar", "gpsimd", "gpsimd")
+        xs_codes = {}
+        raws = {}
 
         def gather_scales(jh):
             v_scales[jh] = keep.tile([P, HALF], U8, name="v_scales%d" % jh, align_bytes=64)
             nc.vector.tensor_copy(v_scales[jh][:], tab_plane[:].indirect(offsets[:, 32 * jh : 32 * (jh + 1)]))
 
         def gather_codes(jh):
-            v_codes[jh] = keep.tile([P, HALF], U32, name="v_codes%d" % jh, tag="half%d" % jh, align_bytes=64)
+            v_codes[jh] = keep.tile([P, HALF], U32, name="v_codes%d" % jh, align_bytes=64)
             nc.vector.tensor_copy(
                 v_codes[jh][:], tab[:].bitcast(U32).indirect(offsets[:, 32 * jh : 32 * (jh + 1)])
             )
 
-        def e_passes(bank, b, q, t, start, stop):
+        def e_passes(bank, b, q, t, start):
             jh, c0 = divmod(q * COLS, HALF)
             for a in range(2):
-                codes, scales = ws_q[b, a]
+                operand, w0 = ws_q[b, a]
+                lhsT, lhsT_scale = columns(operand, w0 + t * P, P)
                 nc.tensor.matmul_mx(
                     out=bank[:, t, :],
-                    lhsT=codes[:, t * P : (t + 1) * P].bitcast(FP8X4),
-                    lhsT_scale=scales[:, t * P : (t + 1) * P],
+                    lhsT=lhsT,
+                    lhsT_scale=lhsT_scale,
                     rhs=xs_codes[jh][:, a, c0 : c0 + COLS].bitcast(FP8X4),
                     rhs_scale=xs_plane[4 * a :, q * COLS : (q + 1) * COLS],
                     start=start and a == 0,
-                    stop=stop and a == 1,
+                    stop=a == 1,
                 )
-
-        def v_pass(bank, lhsT, lhsT_scale, q, t, stop):
-            jh, c0 = divmod(q * COLS, HALF)
-            nc.tensor.matmul_mx(
-                out=bank[:, t, :],
-                lhsT=lhsT,
-                lhsT_scale=lhsT_scale,
-                rhs=v_codes[jh][:, c0 : c0 + COLS].bitcast(FP8X4),
-                rhs_scale=v_scales[jh][:, c0 : c0 + COLS],
-                start=True,
-                stop=stop,
-            )
 
         def woven(bank):
             return bank[:].rearrange("p t n -> p n t")
 
         neg_e = {}
+        diff = {}
         dist = {}
         h_bf = {}
         h_q = {}
@@ -179,100 +160,130 @@ def tile_list_typewriter_strokes_kernel(
         def stage_e(b, q):
             if (b, q) in TWICE:
                 return
-            bank = psum.tile([P, PACK, COLS], F32, name="bank_e")
+            bank = psum.tile([P, PACK, COLS], F32, name="bank_e", tag="single", bufs=4)
             for t in range(PACK):
-                e_passes(bank, b, q, t, True, True)
-            neg_e[b, q] = ring.tile([P, COLS, PACK], F32, name="neg_e", bufs=6)
+                e_passes(bank, b, q, t, True)
+            neg_e[b, q] = ring.tile([P, COLS, PACK], F32, name="neg_e", bufs=5)
             if (b, q) in COPY_ON_VECTOR:
                 nc.vector.tensor_copy(out=neg_e[b, q][:], in_=woven(bank))
             else:
                 nc.scalar.copy(out=neg_e[b, q][:], in_=woven(bank))
 
-        def distance(b, q, side):
+        def difference(b, q, side):
             twice = (b, q) in TWICE
-            bank = psum.tile([P, PACK, COLS], F32, name="bank_" + side)
+            jh, c0 = divmod(q * COLS, HALF)
+            bank = psum.tile([P, PACK, COLS], F32, name="bank_%d" % side)
             for t in range(PACK):
-                if side == "a":
-                    codes, scales = wa_q[b]
-                    lhsT = codes[:, t * P : (t + 1) * P].bitcast(FP8X4)
-                    lhsT_scale = scales[:, t * P : (t + 1) * P]
+                if side == 0:
+                    operand, w0 = wa_q[b]
+                    lhsT, lhsT_scale = columns(operand, w0 + t * P, P)
                 else:
-                    c0 = b * PASS + t * P
-                    lhsT = wb_codes[:, 2 * c0 : 2 * (c0 + P)].bitcast(FP4X4)
-                    lhsT_scale = wb_plane[:, c0 : c0 + P]
-                v_pass(bank, lhsT, lhsT_scale, q, t, not twice)
+                    w0 = b * PASS + t * P
+                    lhsT = wb_codes[:, 2 * w0 : 2 * (w0 + P)].bitcast(FP4X4)
+                    lhsT_scale = wb_plane[:, w0 : w0 + P]
+                nc.tensor.matmul_mx(
+                    out=bank[:, t, :],
+                    lhsT=lhsT,
+                    lhsT_scale=lhsT_scale,
+                    rhs=v_codes[jh][:, c0 : c0 + COLS].bitcast(FP8X4),
+                    rhs_scale=v_scales[jh][:, c0 : c0 + COLS],
+                    start=True,
+                    stop=not twice,
+                )
                 if twice:
-                    e_passes(bank, b, q, t, False, True)
-            dist[b, q, side] = ring.tile([P, COLS, PACK], F32, name="dist_" + side, bufs=5)
+                    e_passes(bank, b, q, t, False)
+            if (b, q) not in dist:
+                dist[b, q] = ring.tile([P, 2, COLS, PACK], F32, name="dist", bufs=7)
+                if not twice:
+                    diff[b, q] = ring.tile([P, 2, COLS, PACK], F32, name="diff", bufs=4)
             if twice:
-                nc.scalar.activation(out=dist[b, q, side][:], in_=woven(bank), func=ACT.Abs)
+                nc.scalar.activation(out=dist[b, q][:, side], in_=woven(bank), func=ACT.Abs)
             else:
-                if (b, q, side) == (0, 0, "b"):
-                    diff = keep.tile([P, COLS, PACK], F32, name="diff_first", tag="half1", align_bytes=64)
-                else:
-                    diff = ring.tile([P, COLS, PACK], F32, name="diff_" + side)
-                nc.vector.tensor_tensor(out=diff[:], in0=woven(bank), in1=neg_e[b, q][:], op=ALU.add)
+                nc.vector.tensor_tensor(out=diff[b, q][:, side], in0=woven(bank), in1=neg_e[b, q][:], op=ALU.add)
+
+        def absolute(b, q, lo, hi):
+            if (b, q) not in TWICE:
                 nc.scalar.activation(
-                    out=dist[b, q, side][:].rearrange("p n t -> p (n t)"),
-                    in_=diff[:].rearrange("p n t -> p (n t)"),
+                    out=dist[b, q][:, lo:hi].rearrange("p u n t -> p (u n t)"),
+                    in_=diff[b, q][:, lo:hi].rearrange("p u n t -> p (u n t)"),
                     func=ACT.Abs,
                 )
 
         def h_piece(b, q):
-            pieces = CHUNKS if b == GROUPS - 1 else ((0, HALF), (HALF, HALF))
-            for j0, width in pieces:
+            for j0, width in CHUNKS[b]:
                 if j0 <= q * COLS < j0 + width:
                     return j0, width
 
         def stage_h(b, q):
-            j0, width = h_piece(b, q)
-            if q * COLS == j0:
-                h_bf[b, j0] = keep.tile([P, PACK * width], BF16, name="h_bf%d_%d" % (b, j0), align_bytes=64)
-            e0 = PACK * (q * COLS - j0)
+            if b not in h_bf:
+                h_bf[b] = keep.tile([P, PACK * S], BF16, name="h_bf%d" % b, tag=("ws1_bf", "h_bf1")[b], align_bytes=64)
+            e0 = PACK * q * COLS
             engine = nc.vector if (b, q) in SUB_ON_VECTOR else nc.gpsimd
-            engine.tensor_tensor(
-                out=h_bf[b, j0][:, e0 : e0 + PASS],
-                in0=dist[b, q, "a"][:].rearrange("p n t -> p (n t)"),
-                in1=dist[b, q, "b"][:].rearrange("p n t -> p (n t)"),
-                op=ALU.subtract,
-            )
+            d = dist[b, q][:].rearrange("p u n t -> p u (n t)")
+            engine.tensor_tensor(out=h_bf[b][:, e0 : e0 + PASS], in0=d[:, 0], in1=d[:, 1], op=ALU.subtract)
 
         def stage_quant(b, q):
             j0, width = h_piece(b, q)
             if (q + 1) * COLS == j0 + width:
-                h_q[b, j0] = quantize("h%d_%d" % (b, j0), h_bf[b, j0][:], width)
+                h_q[b, j0] = quantize("h%d_%d" % (b, j0), h_bf[b][:, PACK * j0 : PACK * (j0 + width)])
 
         def stage_out(q):
             j0, width = h_piece(GROUPS - 1, q)
             if (q + 1) * COLS != j0 + width:
                 return
             result = keep.tile([P, OUT_TILES, width], F32, name="result%d" % j0)
-            for c in range(OUT_TILES):
-                bank = psum.tile([P, HALF], F32, name="bank_y")
+            per_bank = min(OUT_TILES, HALF // width)
+            for c0 in range(0, OUT_TILES, per_bank):
+                tiles = range(c0, min(c0 + per_bank, OUT_TILES))
+                bank = psum.tile([P, HALF], F32, name="bank_y", tag="single", bufs=4)
                 for b in range(GROUPS):
                     p0 = h_piece(b, q)[0]
-                    codes, scales = h_q[b, p0]
-                    cols = slice(j0 - p0, j0 - p0 + width)
-                    w0 = b * N + c * P
-                    nc.tensor.matmul_mx(
-                        out=bank[:, 0:width],
-                        lhsT=wo_codes[:, w0 : w0 + P].bitcast(FP8X4),
-                        lhsT_scale=wo_scales[:, w0 : w0 + P],
-                        rhs=codes[:, cols].bitcast(FP8X4),
-                        rhs_scale=scales[:, cols],
-                        start=b == 0,
-                        stop=b == GROUPS - 1,
+                    rhs, rhs_scale = columns(h_q[b, p0], j0 - p0, width)
+                    for c in tiles:
+                        operand, w0 = wo_q[b * OUT_TILES + c]
+                        lhsT, lhsT_scale = columns(operand, w0, P)
+                        nc.tensor.matmul_mx(
+                            out=bank[:, (c - c0) * width : (c - c0 + 1) * width],
+                            lhsT=lhsT,
+                            lhsT_scale=lhsT_scale,
+                            rhs=rhs,
+                            rhs_scale=rhs_scale,
+                            start=b == 0 and c == tiles[0],
+                            stop=b == GROUPS - 1 and c == tiles[-1],
+                        )
+                for c in tiles:
+                    nc.scalar.activation(
+                        out=result[:, c, :],
+                        in_=bank[:, (c - c0) * width : (c - c0 + 1) * width],
+                        func=ACT.Tanh,
+                        bias=bias[:, c : c + 1],
                     )
-                nc.scalar.activation(
-                    out=result[:, c, :], in_=bank[:, 0:width], func=ACT.Tanh, bias=bias[:, c : c + 1]
-                )
             nc.sync.dma_start(
                 out=out[:, j0 : j0 + width].rearrange("(c p) j -> p c j", p=P), in_=result[:]
             )
 
-        ws_q[0, 0] = weight("ws00", ws_raw[0, 0], -1.0, head)
-        ws_q[0, 1] = weight("ws01", ws_raw[0, 1], -1.0, head)
-        for q in range(4):
+        raws["ws00"] = load_rows(ws, 0, 0)
+        load_plane(xs_plane, xs_scales, 2)
+        xs_codes[0] = load_xs(0)
+        nc.sync.dma_start(offsets[:], offs)
+        raws["ws01"] = load_rows(ws, PASS, 0)
+        load_plane(tab_plane, tab_scales, 1)
+        wb_raw = keep.tile([P, 2 * H], U8, name="wb_raw", align_bytes=64)
+        nc.sync.dma_start(out=wb_raw[:].bitcast(I32), in_=wb_words[0].bitcast(I32))
+        tab = keep.tile([P, T], I32, name="tab", align_bytes=64)
+        nc.sync.dma_start(out=tab[:], in_=tab_words[0].rearrange("p t i -> p (t i)").bitcast(I32))
+        load_plane(wb_plane_raw, wb_scales, 1)
+        raws["wa0"] = load_rows(wa, 0, 0)
+        xs_codes[1] = load_xs(1)
+        raws["ws10"] = load_rows(ws, 0, PASS)
+
+        for a in range(2):
+            grouped = keep.tile([P, PACK * PASS], BF16, name="ws0%d_bf" % a, align_bytes=64)
+            round_weight("ws0%d" % a, grouped[:], raws["ws0%d" % a], -1.0)
+            ws_q[0, a] = quantize("ws0%d" % a, grouped[:]), 0
+        raws["ws11"] = load_rows(ws, PASS, PASS)
+        raws["wa1"] = load_rows(wa, 0, PASS)
+        for q in range(EARLY):
             stage_e(0, q)
         gather_scales(0)
         wb_codes = keep.tile([P, 2 * H], U8, name="wb_codes", align_bytes=64)
@@ -284,49 +295,65 @@ def tile_list_typewriter_strokes_kernel(
             )
         gather_scales(1)
         gather_codes(0)
-        wa_q[0] = weight("wa0", wa_raw[0], 1.0, head_a)
-        for q in range(4):
-            distance(0, q, "b")
+        grouped = keep.tile([P, PACK * PASS], BF16, name="wa0_bf", align_bytes=64)
+        round_weight("wa0", grouped[:], raws["wa0"], 1.0)
+        wa_q[0] = quantize("wa0", grouped[:]), 0
+        raws["wo0"] = load_wo(0)
+        for q in range(EARLY):
+            difference(0, q, 1)
+            absolute(0, q, 1, 2)
         gather_codes(1)
 
-        wo_bf = keep.tile([P, GROUPS, N, PACK], BF16, name="wo_bf", align_bytes=64)
-        wo_codes = keep.tile([P, GROUPS * N], U32, name="wo_codes", align_bytes=64)
-        wo_scales = keep.tile([P, GROUPS * N], U8, name="wo_scales", align_bytes=64)
+        def finish(b, q, now):
+            stage_h(b, q)
+            stage_quant(b, q)
+            if b == GROUPS - 1:
+                if now:
+                    stage_out(q)
+                else:
+                    waiting.append(q)
 
-        steps = [(b, q) for b in range(GROUPS) for q in range(STRIPS)]
-        for k in range(len(steps) + 2):
-            if k >= 2:
-                stage_quant(*steps[k - 2])
-                if steps[k - 2][0] == GROUPS - 1:
-                    stage_out(steps[k - 2][1])
-            if 4 <= k + 2 < len(steps):
-                stage_e(*steps[k + 2])
-            if k < len(steps):
-                distance(*steps[k], "a")
-                if k >= 4:
-                    distance(*steps[k], "b")
-            if 1 <= k <= len(steps):
-                stage_h(*steps[k - 1])
+        waiting = []
+        ws1_bf = keep.tile([P, 2 * PACK * PASS], BF16, name="ws1_bf", align_bytes=64)
+        late_bf = keep.tile([P, PACK * (PASS + GROUPS * N)], BF16, name="late_bf", align_bytes=64)
+        wo0 = PACK * PASS
+        wo1 = wo0 + PACK * N
+
+        finished = 0
+        for k in range(len(STEPS)):
+            if EARLY <= k + 2 < len(STEPS):
+                stage_e(*STEPS[k + 2])
+            difference(*STEPS[k], 0)
+            if k < EARLY:
+                absolute(*STEPS[k], 0, 1)
+            else:
+                difference(*STEPS[k], 1)
+                absolute(*STEPS[k], 0, 2)
+            if k > 2:
+                while finished < k:
+                    finish(*STEPS[finished], k < 15)
+                    finished = finished + 1
+            if k == 1:
+                round_weight("ws10", ws1_bf[:, 0 : PACK * PASS], raws["ws10"], -1.0)
+                raws["wo1"] = load_wo(1)
+                bias = keep.tile([P, OUT_TILES], F32, name="bias")
+                with nc.allow_non_contiguous_dma(reason="one bias value a partition"):
+                    nc.sync.dma_start(out=bias[:], in_=bo.rearrange("(c p) -> p c", p=P))
             if k == 2:
-                ws_q[1, 0] = weight("ws10", ws_raw[1, 0], -1.0, LATE_CASTS[0])
+                round_weight("ws11", ws1_bf[:, PACK * PASS :], raws["ws11"], -1.0)
+                both = quantize("ws1", ws1_bf[:])
+                ws_q[1, 0] = both, 0
+                ws_q[1, 1] = both, PASS
             if k == 3:
-                ws_q[1, 1] = weight("ws11", ws_raw[1, 1], -1.0, LATE_CASTS[1])
+                round_weight("wa1", late_bf[:, 0:wo0], raws["wa1"], 1.0)
+                wa_q[1] = quantize("wa1", late_bf[:, 0:wo0]), 0
             if k == 5:
-                wa_q[1] = weight("wa1", wa_raw[1], 1.0, LATE_CASTS[2])
-            if k == 8:
-                for b in range(GROUPS):
-                    for u in range(2):
-                        cols = slice(u * N // 2, (u + 1) * N // 2)
-                        scale_cast(
-                            LATE_CASTS[3][2 * b + u],
-                            wo_bf[:, b, cols, :],
-                            wo_raw[b][:].rearrange("p t n -> p n t")[:, cols, :],
-                            1.0,
-                        )
-                flat = wo_bf[:].rearrange("p b n t -> p (b n t)")
-                for w0, w1 in ((0, 512), (512, 768)):
-                    nc.vector.quantize_mx(
-                        out=wo_codes[:, w0:w1].bitcast(FP8X4),
-                        scales=wo_scales[:, w0:w1],
-                        in_=flat[:, PACK * w0 : PACK * w1],
-                    )
+                round_wo("wo0", late_bf[:, wo0:wo1], raws["wo0"])
+                round_wo("wo1", late_bf[:, wo1:], raws["wo1"])
+                first = quantize("late0", late_bf[:, wo0 : 2 * wo0])
+                second = quantize("late1", late_bf[:, 2 * wo0 :])
+                for m in range(GROUPS * OUT_TILES):
+                    wo_q[m] = (first, m * P) if m < PACK else (second, (m - PACK) * P)
+        finish(*STEPS[-1], False)
+        for q in waiting:
+            stage_out(q)

@@ -19,20 +19,18 @@ ACT = mybir.ActivationFunctionType
 P = 128
 PACK = 4
 PASS = P * PACK
-BLOCKS = 16
-RUN = 8
+RUN = 4
 GROUPS = H // PASS
-COLS = 128
-STRIPS = S // COLS
+STRIP = 128
+STRIPS = S // STRIP
 HALF = 512
 OUT_TILES = N // P
-EARLY = 4
-CHUNKS = (((0, 512), (512, 512)), ((0, 512), (512, 256), (768, 128), (896, 128)))
-STEPS = ((0, 0), (0, 1), (0, 2), (0, 3), (0, 4), (0, 5), (0, 6), (0, 7), (1, 0), (1, 1), (1, 2), (1, 3), (1, 4), (1, 5), (1, 6), (1, 7), )
-TWICE = ((1, 1), (1, 4), (1, 7), )
-SUB_ON_VECTOR = ((0, 0), (0, 1), (0, 2), (0, 3), (0, 4), (0, 5), (0, 6), (0, 7), (1, 0), (1, 1), (1, 2), (1, 3), (1, 4), (1, 5), (1, 6), (1, 7), )
-COPY_ON_VECTOR = ()
-SHARES = {"ws00": (("vector", 0, 12), ("scalar", 12, 16), ), "ws01": (("vector", 0, 12), ("scalar", 12, 16), ), "wa0": (("scalar", 0, 8), ("gpsimd", 8, 16), ), "ws10": (("gpsimd", 0, 16), ), "ws11": (("gpsimd", 0, 16), ), "wa1": (("scalar", 0, 16), ), "wo0": (("scalar", 0, 16), ), "wo1": (("vector", 0, 16), )}
+SIDE_A, SIDE_B = 0, 1
+
+EARLY = HALF // STRIP
+E_IN_PSUM = ((0, 4), (0, 5), (0, 6), )
+RANGES = (((0, 512), (512, 512)), ((0, 512), (512, 256), (768, 128), (896, 128)))
+SCALAR_SHARE = {"ws_first": 4, "wa0": 8, "ws01": 10, "ws11": 10, "wa1": 8, "wo0": 8, "wo1": 0}
 
 
 def tile_list_typewriter_strokes_kernel(
@@ -41,68 +39,74 @@ def tile_list_typewriter_strokes_kernel(
     nc = tc.nc
     with ExitStack() as ctx:
         keep = ctx.enter_context(tc.tile_pool(name="keep", bufs=1))
-        ring = ctx.enter_context(tc.tile_pool(name="ring", bufs=3))
+        ring = ctx.enter_context(tc.tile_pool(name="ring", bufs=4))
         psum = ctx.enter_context(tc.psum_pool(name="psum", bufs=2))
 
-        offsets = keep.tile([P, S // 16], U16, name="offsets")
-        xs_plane = keep.tile([P, S], U8, name="xs_plane", align_bytes=64)
-        wb_plane_raw = keep.tile([P, H], U8, name="wb_plane_raw", align_bytes=64)
-        tab_plane = keep.tile([P, T], U8, name="tab_plane", align_bytes=64)
-        nc.gpsimd.memset(tab_plane[:].bitcast(I32), 0)
-        nc.vector.memset(xs_plane[:].bitcast(I32), 0)
-        nc.vector.memset(wb_plane_raw[:].bitcast(I32), 0)
+        xs_scale = keep.tile([P, S], U8, name="xs_scale", align_bytes=64)
+        wb_scale_raw = keep.tile([P, H], U8, name="wb_scale_raw", align_bytes=64)
+        tab_scale = keep.tile([P, T], U8, name="tab_scale", align_bytes=64)
+        nc.gpsimd.memset(tab_scale[:].bitcast(I32), 0)
+        nc.vector.memset(xs_scale[:].bitcast(I32), 0)
+        nc.vector.memset(wb_scale_raw[:].bitcast(I32), 0)
+
         warm = keep.tile([P, 2], F32, name="warm")
         nc.vector.memset(warm[:, 0:1], 0.0)
         nc.scalar.activation(out=warm[:, 1:2], in_=warm[:, 0:1], func=ACT.Tanh)
 
-        def load_rows(w, k0, c0):
-            raw = ring.tile([P, PACK, PASS], F32, name="raw", bufs=4)
-            nc.sync.dma_start(
-                out=raw[:], in_=w[k0 : k0 + PASS, c0 : c0 + PASS].rearrange("(p j) c -> p j c", j=PACK)
-            )
+
+        def load_rows(w, a, b):
+            raw = ring.tile([P, PACK, PASS], F32, name="raw")
+            rows = w[a * PASS : (a + 1) * PASS, b * PASS : (b + 1) * PASS]
+            nc.sync.dma_start(out=raw[:], in_=rows.rearrange("(p j) c -> p j c", j=PACK))
             return raw
 
-        def load_xs(jh):
-            words = keep.tile([P, 2, HALF], I32, name="xs_codes%d" % jh, align_bytes=64)
-            src = xs_words.rearrange("a p c i -> p a (c i)")[:, :, 4 * HALF * jh : 4 * HALF * (jh + 1)]
-            nc.sync.dma_start(out=words[:], in_=src.bitcast(I32))
-            return words
-
-        def load_plane(plane, rows, depth):
-            for q in range(4):
-                nc.sync.dma_start(
-                    out=plane[32 * q : 32 * q + 4 * depth, :].bitcast(I32),
-                    in_=rows[:, 4 * q : 4 * q + 4, :].bitcast(I32),
-                )
-
         def load_wo(b):
-            raw = ring.tile([P, PACK, N], F32, name="raw", bufs=4)
-            rows = wo.rearrange("(b g t i) n -> b t g i n", b=GROUPS, g=BLOCKS, t=PACK)
+            raw = ring.tile([P, PACK, N], F32, name="raw")
+            rows = wo.rearrange("(b m t i) n -> b t m i n", b=GROUPS, t=PACK, i=RUN)
             for t in range(PACK):
                 nc.sync.dma_start(out=raw[:, t, :], in_=rows[b, t])
             return raw
 
-        def scale_cast(engine, dst, src, factor):
-            if engine == "vector":
-                nc.vector.tensor_scalar(out=dst, in0=src, scalar1=factor, scalar2=None, op0=ALU.mult)
-            elif engine == "scalar":
-                nc.scalar.activation(out=dst, in_=src, func=ACT.Copy, scale=factor)
-            else:
-                nc.gpsimd.tensor_scalar(
-                    out=dst, in0=src, scalar1=factor, scalar2=0.0, op0=ALU.mult, op1=ALU.add
+        def load_xs(half):
+            words = keep.tile([P, 2, HALF], I32, name="xs_codes%d" % half, align_bytes=64)
+            src = xs_words.rearrange("a p c i -> p a (c i)")
+            src = src[:, :, PACK * HALF * half : PACK * HALF * (half + 1)]
+            nc.sync.dma_start(out=words[:], in_=src.bitcast(I32))
+            return words
+
+        def load_scales(tile, rows):
+            for quad in range(4):
+                nc.sync.dma_start(
+                    out=tile[32 * quad : 32 * quad + 4 * rows.shape[0], :].bitcast(I32),
+                    in_=rows[:, 4 * quad : 4 * quad + 4, :].bitcast(I32),
                 )
 
-        def round_weight(name, grouped, raw, factor):
-            src = raw[:].rearrange("p j (g t i) -> p g t i j", t=PACK, i=RUN)
-            dst = grouped.rearrange("p (t g i j) -> p g t i j", t=PACK, i=RUN, j=PACK)
-            for engine, g0, g1 in SHARES[name]:
-                scale_cast(engine, dst[:, g0:g1], src[:, g0:g1], factor)
+
+        def round_negated(name, raw, other):
+            grouped = keep.tile([P, PACK * PASS], BF16, name="ws%d0_bf" % other, align_bytes=64)
+            src = raw[:].rearrange("p j (m t i) -> p m t i j", t=PACK, i=RUN)
+            dst = grouped[:].rearrange("p (t m i j) -> p m t i j", t=PACK, i=RUN, j=PACK)
+            cut = 2 * SCALAR_SHARE[name]
+            nc.scalar.activation(out=dst[:, :cut], in_=src[:, :cut], func=ACT.Copy, scale=-1.0)
+            nc.vector.tensor_scalar(out=dst[:, cut:], in0=src[:, cut:], scalar1=-1.0, scalar2=None, op0=ALU.mult)
+            return grouped
+
+        def copy_shared(name, dst, src):
+            cut = dst.shape[1] * SCALAR_SHARE[name] // 16
+            if cut > 0:
+                nc.scalar.copy(out=dst[:, :cut], in_=src[:, :cut])
+            if cut < dst.shape[1]:
+                nc.vector.tensor_copy(out=dst[:, cut:], in_=src[:, cut:])
+
+        def round_weight(name, grouped, raw):
+            src = raw[:].rearrange("p j (m t i) -> p m t j i", t=PACK, i=RUN)
+            dst = grouped.rearrange("p (t m i j) -> p m t j i", t=PACK, i=RUN, j=PACK)
+            copy_shared(name, dst, src)
 
         def round_wo(name, grouped, raw):
-            src = raw[:].rearrange("p t (g n) -> p g n t", g=BLOCKS)
-            dst = grouped.rearrange("p (g n t) -> p g n t", g=BLOCKS, t=PACK)
-            for engine, g0, g1 in SHARES[name]:
-                scale_cast(engine, dst[:, g0:g1], src[:, g0:g1], 1.0)
+            src = raw[:].rearrange("p t (m i) -> p m t i", i=RUN)
+            dst = grouped.rearrange("p (m i t) -> p m t i", i=RUN, t=PACK)
+            copy_shared(name, dst, src)
 
         def quantize(name, grouped):
             width = grouped.shape[1] // PACK
@@ -115,26 +119,23 @@ def tile_list_typewriter_strokes_kernel(
             codes, scales = operand
             return codes[:, c0 : c0 + width].bitcast(FP8X4), scales[:, c0 : c0 + width]
 
-        ws_q = {}
-        wa_q = {}
-        wo_q = {}
-        v_codes = {}
-        v_scales = {}
-        xs_codes = {}
-        raws = {}
+        def list_half(half):
+            return offsets[:, half * HALF // 16 : (half + 1) * HALF // 16]
 
-        def gather_scales(jh):
-            v_scales[jh] = keep.tile([P, HALF], U8, name="v_scales%d" % jh, align_bytes=64)
-            nc.vector.tensor_copy(v_scales[jh][:], tab_plane[:].indirect(offsets[:, 32 * jh : 32 * (jh + 1)]))
+        def gather_scales(half):
+            v_scales[half] = keep.tile([P, HALF], U8, name="v_scales%d" % half, align_bytes=64)
+            nc.vector.tensor_copy(v_scales[half][:], tab_scale[:].indirect(list_half(half)))
 
-        def gather_codes(jh):
-            v_codes[jh] = keep.tile([P, HALF], U32, name="v_codes%d" % jh, align_bytes=64)
-            nc.vector.tensor_copy(
-                v_codes[jh][:], tab[:].bitcast(U32).indirect(offsets[:, 32 * jh : 32 * (jh + 1)])
-            )
+        def gather_codes(half):
+            v_codes[half] = keep.tile([P, HALF], U32, name="v_codes%d" % half, align_bytes=64)
+            nc.vector.tensor_copy(v_codes[half][:], tab[:].bitcast(U32).indirect(list_half(half)))
+
+
+        def woven(bank):
+            return bank[:].rearrange("p t n -> p n t")
 
         def e_passes(bank, b, q, t, start):
-            jh, c0 = divmod(q * COLS, HALF)
+            half, c0 = divmod(q * STRIP, HALF)
             for a in range(2):
                 operand, w0 = ws_q[b, a]
                 lhsT, lhsT_scale = columns(operand, w0 + t * P, P)
@@ -142,94 +143,82 @@ def tile_list_typewriter_strokes_kernel(
                     out=bank[:, t, :],
                     lhsT=lhsT,
                     lhsT_scale=lhsT_scale,
-                    rhs=xs_codes[jh][:, a, c0 : c0 + COLS].bitcast(FP8X4),
-                    rhs_scale=xs_plane[4 * a :, q * COLS : (q + 1) * COLS],
+                    rhs=xs_codes[half][:, a, c0 : c0 + STRIP].bitcast(FP8X4),
+                    rhs_scale=xs_scale[4 * a :, q * STRIP : (q + 1) * STRIP],
                     start=start and a == 0,
                     stop=a == 1,
                 )
 
-        def woven(bank):
-            return bank[:].rearrange("p t n -> p n t")
-
-        neg_e = {}
-        diff = {}
-        dist = {}
-        h_bf = {}
-        h_q = {}
-
-        def stage_e(b, q):
-            if (b, q) in TWICE:
+        def strokes(b, q):
+            if (b, q) in E_IN_PSUM:
                 return
-            bank = psum.tile([P, PACK, COLS], F32, name="bank_e", tag="single", bufs=4)
+            bank = psum.tile([P, PACK, STRIP], F32, name="bank_e", tag="single", bufs=4)
             for t in range(PACK):
                 e_passes(bank, b, q, t, True)
-            neg_e[b, q] = ring.tile([P, COLS, PACK], F32, name="neg_e", bufs=5)
-            if (b, q) in COPY_ON_VECTOR:
-                nc.vector.tensor_copy(out=neg_e[b, q][:], in_=woven(bank))
-            else:
-                nc.scalar.copy(out=neg_e[b, q][:], in_=woven(bank))
+            e_sb[b, q] = ring.tile([P, STRIP, PACK], F32, name="e_sb", bufs=6)
+            nc.scalar.copy(out=e_sb[b, q][:], in_=woven(bank))
 
         def difference(b, q, side):
-            twice = (b, q) in TWICE
-            jh, c0 = divmod(q * COLS, HALF)
-            bank = psum.tile([P, PACK, COLS], F32, name="bank_%d" % side)
+            fused = (b, q) in E_IN_PSUM
+            half, c0 = divmod(q * STRIP, HALF)
+            bank = psum.tile([P, PACK, STRIP], F32, name="bank_%d" % side)
             for t in range(PACK):
-                if side == 0:
-                    operand, w0 = wa_q[b]
-                    lhsT, lhsT_scale = columns(operand, w0 + t * P, P)
+                if side == SIDE_A:
+                    lhsT, lhsT_scale = columns(wa_q[b], t * P, P)
                 else:
                     w0 = b * PASS + t * P
                     lhsT = wb_codes[:, 2 * w0 : 2 * (w0 + P)].bitcast(FP4X4)
-                    lhsT_scale = wb_plane[:, w0 : w0 + P]
+                    lhsT_scale = wb_scale[:, w0 : w0 + P]
                 nc.tensor.matmul_mx(
                     out=bank[:, t, :],
                     lhsT=lhsT,
                     lhsT_scale=lhsT_scale,
-                    rhs=v_codes[jh][:, c0 : c0 + COLS].bitcast(FP8X4),
-                    rhs_scale=v_scales[jh][:, c0 : c0 + COLS],
+                    rhs=v_codes[half][:, c0 : c0 + STRIP].bitcast(FP8X4),
+                    rhs_scale=v_scales[half][:, c0 : c0 + STRIP],
                     start=True,
-                    stop=not twice,
+                    stop=not fused,
                 )
-                if twice:
+                if fused:
                     e_passes(bank, b, q, t, False)
-            if (b, q) not in dist:
-                dist[b, q] = ring.tile([P, 2, COLS, PACK], F32, name="dist", bufs=7)
-                if not twice:
-                    diff[b, q] = ring.tile([P, 2, COLS, PACK], F32, name="diff", bufs=4)
-            if twice:
-                nc.scalar.activation(out=dist[b, q][:, side], in_=woven(bank), func=ACT.Abs)
-            else:
-                nc.vector.tensor_tensor(out=diff[b, q][:, side], in0=woven(bank), in1=neg_e[b, q][:], op=ALU.add)
+            if (b, q // 2) not in dist:
+                dist[b, q // 2] = ring.tile([P, 2, 2, STRIP, PACK], F32, name="dist", bufs=3)
+            if fused:
+                nc.scalar.activation(out=dist[b, q // 2][:, q % 2, side], in_=woven(bank), func=ACT.Abs)
+                return
+            if (b, q) not in diff:
+                diff[b, q] = ring.tile([P, 2, STRIP, PACK], F32, name="diff", bufs=4)
+            op = ALU.add if b == 0 else ALU.subtract
+            nc.vector.tensor_tensor(out=diff[b, q][:, side], in0=woven(bank), in1=e_sb[b, q][:], op=op)
 
-        def absolute(b, q, lo, hi):
-            if (b, q) not in TWICE:
+        def absolute(b, q, side0, side1):
+            if (b, q) not in E_IN_PSUM:
                 nc.scalar.activation(
-                    out=dist[b, q][:, lo:hi].rearrange("p u n t -> p (u n t)"),
-                    in_=diff[b, q][:, lo:hi].rearrange("p u n t -> p (u n t)"),
+                    out=dist[b, q // 2][:, q % 2, side0:side1].rearrange("p u n t -> p (u n t)"),
+                    in_=diff[b, q][:, side0:side1].rearrange("p u n t -> p (u n t)"),
                     func=ACT.Abs,
                 )
 
-        def h_piece(b, q):
-            for j0, width in CHUNKS[b]:
-                if j0 <= q * COLS < j0 + width:
-                    return j0, width
+        def range_of(b, q):
+            return [r for r in RANGES[b] if r[0] <= q * STRIP < r[0] + r[1]][0]
 
-        def stage_h(b, q):
-            if b not in h_bf:
-                h_bf[b] = keep.tile([P, PACK * S], BF16, name="h_bf%d" % b, tag=("ws1_bf", "h_bf1")[b], align_bytes=64)
-            e0 = PACK * q * COLS
-            engine = nc.vector if (b, q) in SUB_ON_VECTOR else nc.gpsimd
-            d = dist[b, q][:].rearrange("p u n t -> p u (n t)")
-            engine.tensor_tensor(out=h_bf[b][:, e0 : e0 + PASS], in0=d[:, 0], in1=d[:, 1], op=ALU.subtract)
-
-        def stage_quant(b, q):
-            j0, width = h_piece(b, q)
-            if (q + 1) * COLS == j0 + width:
+        def subtract_and_quantize(b, q):
+            j0, width = range_of(b, q)
+            if width > STRIP and q % 2 == 0:
+                return
+            first = q if width == STRIP else q - 1
+            pair = dist[b, q // 2][:, first % 2 : q % 2 + 1].rearrange("p s u n t -> p s u (n t)")
+            nc.vector.tensor_tensor(
+                out=h_bf[b][:, first * PASS : (q + 1) * PASS].rearrange("p (s c) -> p s c", c=PASS),
+                in0=pair[:, :, SIDE_A],
+                in1=pair[:, :, SIDE_B],
+                op=ALU.subtract,
+            )
+            if (q + 1) * STRIP == j0 + width:
                 h_q[b, j0] = quantize("h%d_%d" % (b, j0), h_bf[b][:, PACK * j0 : PACK * (j0 + width)])
 
-        def stage_out(q):
-            j0, width = h_piece(GROUPS - 1, q)
-            if (q + 1) * COLS != j0 + width:
+        def scores(q):
+            j0, width = range_of(GROUPS - 1, q)
+            if (q + 1) * STRIP != j0 + width:
                 return
             result = keep.tile([P, OUT_TILES, width], F32, name="result%d" % j0)
             per_bank = min(OUT_TILES, HALF // width)
@@ -237,11 +226,10 @@ def tile_list_typewriter_strokes_kernel(
                 tiles = range(c0, min(c0 + per_bank, OUT_TILES))
                 bank = psum.tile([P, HALF], F32, name="bank_y", tag="single", bufs=4)
                 for b in range(GROUPS):
-                    p0 = h_piece(b, q)[0]
-                    rhs, rhs_scale = columns(h_q[b, p0], j0 - p0, width)
+                    h0 = range_of(b, q)[0]
+                    rhs, rhs_scale = columns(h_q[b, h0], j0 - h0, width)
                     for c in tiles:
-                        operand, w0 = wo_q[b * OUT_TILES + c]
-                        lhsT, lhsT_scale = columns(operand, w0, P)
+                        lhsT, lhsT_scale = columns(*wo_q[b * OUT_TILES + c], P)
                         nc.tensor.matmul_mx(
                             out=bank[:, (c - c0) * width : (c - c0 + 1) * width],
                             lhsT=lhsT,
@@ -258,102 +246,93 @@ def tile_list_typewriter_strokes_kernel(
                         func=ACT.Tanh,
                         bias=bias[:, c : c + 1],
                     )
-            nc.sync.dma_start(
-                out=out[:, j0 : j0 + width].rearrange("(c p) j -> p c j", p=P), in_=result[:]
-            )
+            nc.sync.dma_start(out=out[:, j0 : j0 + width].rearrange("(c p) j -> p c j", p=P), in_=result[:])
 
-        raws["ws00"] = load_rows(ws, 0, 0)
-        load_plane(xs_plane, xs_scales, 2)
+        xs_codes, v_codes, v_scales = {}, {}, {}
+        ws_q, wa_q, wo_q, h_q = {}, {}, {}, {}
+        e_sb, diff, dist = {}, {}, {}
+
+        ws00 = load_rows(ws, 0, 0)
+        load_scales(xs_scale, xs_scales)
         xs_codes[0] = load_xs(0)
+        offsets = keep.tile([P, S // 16], U16, name="offsets")
         nc.sync.dma_start(offsets[:], offs)
-        raws["ws01"] = load_rows(ws, PASS, 0)
-        load_plane(tab_plane, tab_scales, 1)
+        ws10 = load_rows(ws, 1, 0)
+        load_scales(tab_scale, tab_scales)
         wb_raw = keep.tile([P, 2 * H], U8, name="wb_raw", align_bytes=64)
         nc.sync.dma_start(out=wb_raw[:].bitcast(I32), in_=wb_words[0].bitcast(I32))
         tab = keep.tile([P, T], I32, name="tab", align_bytes=64)
         nc.sync.dma_start(out=tab[:], in_=tab_words[0].rearrange("p t i -> p (t i)").bitcast(I32))
-        load_plane(wb_plane_raw, wb_scales, 1)
-        raws["wa0"] = load_rows(wa, 0, 0)
+        load_scales(wb_scale_raw, wb_scales)
+        wa0 = load_rows(wa, 0, 0)
         xs_codes[1] = load_xs(1)
-        raws["ws10"] = load_rows(ws, 0, PASS)
+        ws01 = load_rows(ws, 0, 1)
 
-        for a in range(2):
-            grouped = keep.tile([P, PACK * PASS], BF16, name="ws0%d_bf" % a, align_bytes=64)
-            round_weight("ws0%d" % a, grouped[:], raws["ws0%d" % a], -1.0)
-            ws_q[0, a] = quantize("ws0%d" % a, grouped[:]), 0
-        raws["ws11"] = load_rows(ws, PASS, PASS)
-        raws["wa1"] = load_rows(wa, 0, PASS)
+        for a, raw in enumerate((ws00, ws10)):
+            ws_q[0, a] = quantize("ws%d0" % a, round_negated("ws_first", raw, a)[:]), 0
+        ws11 = load_rows(ws, 1, 1)
+        wa1 = load_rows(wa, 0, 1)
         for q in range(EARLY):
-            stage_e(0, q)
+            strokes(0, q)
         gather_scales(0)
         wb_codes = keep.tile([P, 2 * H], U8, name="wb_codes", align_bytes=64)
-        wb_plane = keep.tile([P, H], U8, name="wb_plane", align_bytes=64)
-        for dst, src, words in ((wb_codes, wb_raw, 4), (wb_plane, wb_plane_raw, 2)):
+        wb_scale = keep.tile([P, H], U8, name="wb_scale", align_bytes=64)
+        for dst, src, words in ((wb_codes, wb_raw, 2), (wb_scale, wb_scale_raw, 1)):
             nc.vector.tensor_copy(
-                out=dst[:].bitcast(I32).rearrange("p (b t g w) -> p b t g w", b=GROUPS, t=PACK, w=words),
-                in_=src[:].bitcast(I32).rearrange("p (b g t w) -> p b t g w", b=GROUPS, t=PACK, w=words),
+                out=dst[:].bitcast(I32).rearrange("p (b t m w) -> p b t m w", b=GROUPS, t=PACK, w=words),
+                in_=src[:].bitcast(I32).rearrange("p (b m t w) -> p b t m w", b=GROUPS, t=PACK, w=words),
             )
         gather_scales(1)
         gather_codes(0)
-        grouped = keep.tile([P, PACK * PASS], BF16, name="wa0_bf", align_bytes=64)
-        round_weight("wa0", grouped[:], raws["wa0"], 1.0)
-        wa_q[0] = quantize("wa0", grouped[:]), 0
-        raws["wo0"] = load_wo(0)
+        wa0_bf = keep.tile([P, PACK * PASS], BF16, name="wa0_bf", align_bytes=64)
+        round_weight("wa0", wa0_bf[:], wa0)
+        wa_q[0] = quantize("wa0", wa0_bf[:])
+        wo0 = load_wo(0)
         for q in range(EARLY):
-            difference(0, q, 1)
-            absolute(0, q, 1, 2)
+            difference(0, q, SIDE_B)
+            absolute(0, q, SIDE_B, SIDE_B + 1)
         gather_codes(1)
 
-        def finish(b, q, now):
-            stage_h(b, q)
-            stage_quant(b, q)
-            if b == GROUPS - 1:
-                if now:
-                    stage_out(q)
-                else:
-                    waiting.append(q)
-
-        waiting = []
+        h_bf = [keep.tile([P, PACK * S], BF16, name="h_bf%d" % b, align_bytes=64) for b in range(GROUPS)]
         ws1_bf = keep.tile([P, 2 * PACK * PASS], BF16, name="ws1_bf", align_bytes=64)
-        late_bf = keep.tile([P, PACK * (PASS + GROUPS * N)], BF16, name="late_bf", align_bytes=64)
-        wo0 = PACK * PASS
-        wo1 = wo0 + PACK * N
+        wa1_bf = keep.tile([P, PACK * PASS], BF16, name="wa1_bf", align_bytes=64)
+        wo_bf = keep.tile([P, GROUPS * PACK * N], BF16, name="wo_bf", align_bytes=64)
 
-        finished = 0
-        for k in range(len(STEPS)):
-            if EARLY <= k + 2 < len(STEPS):
-                stage_e(*STEPS[k + 2])
-            difference(*STEPS[k], 0)
+        steps = [(b, q) for b in range(GROUPS) for q in range(STRIPS)]
+        for k, (b, q) in enumerate(steps):
+            if EARLY <= k + 2 < len(steps):
+                strokes(*steps[k + 2])
+            difference(b, q, SIDE_A)
             if k < EARLY:
-                absolute(*STEPS[k], 0, 1)
+                absolute(b, q, SIDE_A, SIDE_A + 1)
             else:
-                difference(*STEPS[k], 1)
-                absolute(*STEPS[k], 0, 2)
-            if k > 2:
-                while finished < k:
-                    finish(*STEPS[finished], k < 15)
-                    finished = finished + 1
+                difference(b, q, SIDE_B)
+                absolute(b, q, SIDE_A, SIDE_B + 1)
+            if k > 0:
+                subtract_and_quantize(*steps[k - 1])
+            if STRIPS < k < 15:
+                scores(q - 1)
             if k == 1:
-                round_weight("ws10", ws1_bf[:, 0 : PACK * PASS], raws["ws10"], -1.0)
-                raws["wo1"] = load_wo(1)
+                round_weight("ws01", ws1_bf[:, : PACK * PASS], ws01)
+                wo1 = load_wo(1)
                 bias = keep.tile([P, OUT_TILES], F32, name="bias")
                 with nc.allow_non_contiguous_dma(reason="one bias value a partition"):
                     nc.sync.dma_start(out=bias[:], in_=bo.rearrange("(c p) -> p c", p=P))
             if k == 2:
-                round_weight("ws11", ws1_bf[:, PACK * PASS :], raws["ws11"], -1.0)
+                round_weight("ws11", ws1_bf[:, PACK * PASS :], ws11)
                 both = quantize("ws1", ws1_bf[:])
                 ws_q[1, 0] = both, 0
                 ws_q[1, 1] = both, PASS
-            if k == 3:
-                round_weight("wa1", late_bf[:, 0:wo0], raws["wa1"], 1.0)
-                wa_q[1] = quantize("wa1", late_bf[:, 0:wo0]), 0
-            if k == 5:
-                round_wo("wo0", late_bf[:, wo0:wo1], raws["wo0"])
-                round_wo("wo1", late_bf[:, wo1:], raws["wo1"])
-                first = quantize("late0", late_bf[:, wo0 : 2 * wo0])
-                second = quantize("late1", late_bf[:, 2 * wo0 :])
+            if k == 4:
+                round_weight("wa1", wa1_bf[:], wa1)
+                wa_q[1] = quantize("wa1", wa1_bf[:])
+            if k == 7:
+                round_wo("wo0", wo_bf[:, : PACK * N], wo0)
+                round_wo("wo1", wo_bf[:, PACK * N :], wo1)
+                front = quantize("wo_front", wo_bf[:, : PACK * PASS])
+                back = quantize("wo_back", wo_bf[:, PACK * PASS :])
                 for m in range(GROUPS * OUT_TILES):
-                    wo_q[m] = (first, m * P) if m < PACK else (second, (m - PACK) * P)
-        finish(*STEPS[-1], False)
-        for q in waiting:
-            stage_out(q)
+                    wo_q[m] = (front, m * P) if m < PACK else (back, (m - PACK) * P)
+        subtract_and_quantize(*steps[-1])
+        for q in range(15 - STRIPS - 1, STRIPS):
+            scores(q)

@@ -28,9 +28,9 @@ OUT_TILES = N // P
 SIDE_A, SIDE_B = 0, 1
 
 EARLY = HALF // STRIP
-E_IN_PSUM = ((0, 4), (0, 5), (0, 6), )
+E_IN_PSUM = ((0, 5), (0, 6), (0, 7), )
 RANGES = (((0, 512), (512, 512)), ((0, 512), (512, 256), (768, 128), (896, 128)))
-SCALAR_SHARE = {"ws_first": 4, "wa0": 8, "ws01": 10, "ws11": 10, "wa1": 8, "wo0": 8, "wo1": 0}
+SCALAR_SHARE = {"ws_first": 4, "wa0": 8, "ws01": 8, "ws11": 8, "wa1": 8, "wo0": 8, "wo1": 8}
 
 
 def tile_list_typewriter_strokes_kernel(
@@ -45,12 +45,12 @@ def tile_list_typewriter_strokes_kernel(
         xs_scale = keep.tile([P, S], U8, name="xs_scale", align_bytes=64)
         wb_scale_raw = keep.tile([P, H], U8, name="wb_scale_raw", align_bytes=64)
         tab_scale = keep.tile([P, T], U8, name="tab_scale", align_bytes=64)
-        nc.gpsimd.memset(tab_scale[:].bitcast(I32), 0)
-        nc.vector.memset(xs_scale[:].bitcast(I32), 0)
-        nc.vector.memset(wb_scale_raw[:].bitcast(I32), 0)
+        nc.gpsimd.memset(xs_scale[:].bitcast(I32), 0)
+        nc.vector.memset(tab_scale[:].bitcast(I32), 0)
+        nc.gpsimd.memset(wb_scale_raw[:].bitcast(I32), 0)
 
         warm = keep.tile([P, 2], F32, name="warm")
-        nc.vector.memset(warm[:, 0:1], 0.0)
+        nc.gpsimd.memset(warm[:, 0:1], 0.0)
         nc.scalar.activation(out=warm[:, 1:2], in_=warm[:, 0:1], func=ACT.Tanh)
 
 

@@ -28,9 +28,11 @@ OUT_TILES = N // P
 SIDE_A, SIDE_B = 0, 1
 
 EARLY = HALF // STRIP
-E_IN_PSUM = ((0, 5), (0, 6), (0, 7), )
+E_IN_PSUM = ((0, STRIPS - 3), (0, STRIPS - 2), (0, STRIPS - 1))
 RANGES = (((0, 512), (512, 512)), ((0, 512), (512, 256), (768, 128), (896, 128)))
-SCALAR_SHARE = {"ws_first": 4, "wa0": 8, "ws01": 8, "ws11": 8, "wa1": 8, "wo0": 8, "wo1": 8}
+E_AHEAD = 2
+ROUND_WS01, ROUND_WS11, ROUND_WA1, ROUND_WO = 1, 2, 4, 7
+E_BUFS, DIST_BUFS, SHARED_BANKS = EARLY + E_AHEAD, 3, 4
 
 
 def tile_list_typewriter_strokes_kernel(
@@ -48,10 +50,6 @@ def tile_list_typewriter_strokes_kernel(
         nc.gpsimd.memset(xs_scale[:].bitcast(I32), 0)
         nc.vector.memset(tab_scale[:].bitcast(I32), 0)
         nc.gpsimd.memset(wb_scale_raw[:].bitcast(I32), 0)
-
-        warm = keep.tile([P, 2], F32, name="warm")
-        nc.gpsimd.memset(warm[:, 0:1], 0.0)
-        nc.scalar.activation(out=warm[:, 1:2], in_=warm[:, 0:1], func=ACT.Tanh)
 
 
         def load_rows(w, a, b):
@@ -82,31 +80,31 @@ def tile_list_typewriter_strokes_kernel(
                 )
 
 
-        def round_negated(name, raw, other):
-            grouped = keep.tile([P, PACK * PASS], BF16, name="ws%d0_bf" % other, align_bytes=64)
+        def round_negated(a, raw):
+            grouped = keep.tile([P, PACK * PASS], BF16, name="ws%d0_bf" % a, align_bytes=64)
             src = raw[:].rearrange("p j (m t i) -> p m t i j", t=PACK, i=RUN)
             dst = grouped[:].rearrange("p (t m i j) -> p m t i j", t=PACK, i=RUN, j=PACK)
-            cut = 2 * SCALAR_SHARE[name]
+            cut = dst.shape[1] // 4
             nc.scalar.activation(out=dst[:, :cut], in_=src[:, :cut], func=ACT.Copy, scale=-1.0)
-            nc.vector.tensor_scalar(out=dst[:, cut:], in0=src[:, cut:], scalar1=-1.0, scalar2=None, op0=ALU.mult)
+            nc.vector.tensor_scalar(
+                out=dst[:, cut:], in0=src[:, cut:], scalar1=-1.0, scalar2=None, op0=ALU.mult
+            )
             return grouped
 
-        def copy_shared(name, dst, src):
-            cut = dst.shape[1] * SCALAR_SHARE[name] // 16
-            if cut > 0:
-                nc.scalar.copy(out=dst[:, :cut], in_=src[:, :cut])
-            if cut < dst.shape[1]:
-                nc.vector.tensor_copy(out=dst[:, cut:], in_=src[:, cut:])
+        def copy_in_halves(dst, src):
+            cut = dst.shape[1] // 2
+            nc.scalar.copy(out=dst[:, :cut], in_=src[:, :cut])
+            nc.vector.tensor_copy(out=dst[:, cut:], in_=src[:, cut:])
 
-        def round_weight(name, grouped, raw):
+        def round_weight(grouped, raw):
             src = raw[:].rearrange("p j (m t i) -> p m t j i", t=PACK, i=RUN)
             dst = grouped.rearrange("p (t m i j) -> p m t j i", t=PACK, i=RUN, j=PACK)
-            copy_shared(name, dst, src)
+            copy_in_halves(dst, src)
 
-        def round_wo(name, grouped, raw):
+        def round_wo(grouped, raw):
             src = raw[:].rearrange("p t (m i) -> p m t i", i=RUN)
             dst = grouped.rearrange("p (m i t) -> p m t i", i=RUN, t=PACK)
-            copy_shared(name, dst, src)
+            copy_in_halves(dst, src)
 
         def quantize(name, grouped):
             width = grouped.shape[1] // PACK
@@ -134,6 +132,9 @@ def tile_list_typewriter_strokes_kernel(
         def woven(bank):
             return bank[:].rearrange("p t n -> p n t")
 
+        def paired(bank):
+            return bank[:].rearrange("p t (n i) -> p n t i", i=2)
+
         def e_passes(bank, b, q, t, start):
             half, c0 = divmod(q * STRIP, HALF)
             for a in range(2):
@@ -152,11 +153,11 @@ def tile_list_typewriter_strokes_kernel(
         def strokes(b, q):
             if (b, q) in E_IN_PSUM:
                 return
-            bank = psum.tile([P, PACK, STRIP], F32, name="bank_e", tag="single", bufs=4)
+            bank = psum.tile([P, PACK, STRIP], F32, name="bank_e", tag="single", bufs=SHARED_BANKS)
             for t in range(PACK):
                 e_passes(bank, b, q, t, True)
-            e_sb[b, q] = ring.tile([P, STRIP, PACK], F32, name="e_sb", bufs=6)
-            nc.scalar.copy(out=e_sb[b, q][:], in_=woven(bank))
+            e_sb[b, q] = ring.tile([P, STRIP // 2, PACK, 2], F32, name="e_sb", bufs=E_BUFS)
+            nc.scalar.copy(out=e_sb[b, q][:], in_=paired(bank))
 
         def difference(b, q, side):
             fused = (b, q) in E_IN_PSUM
@@ -181,20 +182,20 @@ def tile_list_typewriter_strokes_kernel(
                 if fused:
                     e_passes(bank, b, q, t, False)
             if (b, q // 2) not in dist:
-                dist[b, q // 2] = ring.tile([P, 2, 2, STRIP, PACK], F32, name="dist", bufs=3)
+                dist[b, q // 2] = ring.tile([P, 2, 2, STRIP, PACK], F32, name="dist", bufs=DIST_BUFS)
             if fused:
                 nc.scalar.activation(out=dist[b, q // 2][:, q % 2, side], in_=woven(bank), func=ACT.Abs)
                 return
             if (b, q) not in diff:
-                diff[b, q] = ring.tile([P, 2, STRIP, PACK], F32, name="diff", bufs=4)
+                diff[b, q] = ring.tile([P, 2, STRIP // 2, PACK, 2], F32, name="diff")
             op = ALU.add if b == 0 else ALU.subtract
-            nc.vector.tensor_tensor(out=diff[b, q][:, side], in0=woven(bank), in1=e_sb[b, q][:], op=op)
+            nc.vector.tensor_tensor(out=diff[b, q][:, side], in0=paired(bank), in1=e_sb[b, q][:], op=op)
 
         def absolute(b, q, side0, side1):
             if (b, q) not in E_IN_PSUM:
                 nc.scalar.activation(
-                    out=dist[b, q // 2][:, q % 2, side0:side1].rearrange("p u n t -> p (u n t)"),
-                    in_=diff[b, q][:, side0:side1].rearrange("p u n t -> p (u n t)"),
+                    out=dist[b, q // 2][:, q % 2, side0:side1].rearrange("p u (n i) t -> p (u n) i t", i=2),
+                    in_=diff[b, q][:, side0:side1].rearrange("p u n t i -> p (u n) i t"),
                     func=ACT.Abs,
                 )
 
@@ -224,7 +225,7 @@ def tile_list_typewriter_strokes_kernel(
             per_bank = min(OUT_TILES, HALF // width)
             for c0 in range(0, OUT_TILES, per_bank):
                 tiles = range(c0, min(c0 + per_bank, OUT_TILES))
-                bank = psum.tile([P, HALF], F32, name="bank_y", tag="single", bufs=4)
+                bank = psum.tile([P, HALF], F32, name="bank_y", tag="single", bufs=SHARED_BANKS)
                 for b in range(GROUPS):
                     h0 = range_of(b, q)[0]
                     rhs, rhs_scale = columns(h_q[b, h0], j0 - h0, width)
@@ -269,7 +270,7 @@ def tile_list_typewriter_strokes_kernel(
         ws01 = load_rows(ws, 0, 1)
 
         for a, raw in enumerate((ws00, ws10)):
-            ws_q[0, a] = quantize("ws%d0" % a, round_negated("ws_first", raw, a)[:]), 0
+            ws_q[0, a] = quantize("ws%d0" % a, round_negated(a, raw)[:]), 0
         ws11 = load_rows(ws, 1, 1)
         wa1 = load_rows(wa, 0, 1)
         for q in range(EARLY):
@@ -285,7 +286,7 @@ def tile_list_typewriter_strokes_kernel(
         gather_scales(1)
         gather_codes(0)
         wa0_bf = keep.tile([P, PACK * PASS], BF16, name="wa0_bf", align_bytes=64)
-        round_weight("wa0", wa0_bf[:], wa0)
+        round_weight(wa0_bf[:], wa0)
         wa_q[0] = quantize("wa0", wa0_bf[:])
         wo0 = load_wo(0)
         for q in range(EARLY):
@@ -300,8 +301,8 @@ def tile_list_typewriter_strokes_kernel(
 
         steps = [(b, q) for b in range(GROUPS) for q in range(STRIPS)]
         for k, (b, q) in enumerate(steps):
-            if EARLY <= k + 2 < len(steps):
-                strokes(*steps[k + 2])
+            if EARLY <= k + E_AHEAD < len(steps):
+                strokes(*steps[k + E_AHEAD])
             difference(b, q, SIDE_A)
             if k < EARLY:
                 absolute(b, q, SIDE_A, SIDE_A + 1)
@@ -310,29 +311,29 @@ def tile_list_typewriter_strokes_kernel(
                 absolute(b, q, SIDE_A, SIDE_B + 1)
             if k > 0:
                 subtract_and_quantize(*steps[k - 1])
-            if STRIPS < k < 15:
+            if STRIPS < k < len(steps) - 1:
                 scores(q - 1)
-            if k == 1:
-                round_weight("ws01", ws1_bf[:, : PACK * PASS], ws01)
+            if k == ROUND_WS01:
+                round_weight(ws1_bf[:, : PACK * PASS], ws01)
                 wo1 = load_wo(1)
                 bias = keep.tile([P, OUT_TILES], F32, name="bias")
                 with nc.allow_non_contiguous_dma(reason="one bias value a partition"):
                     nc.sync.dma_start(out=bias[:], in_=bo.rearrange("(c p) -> p c", p=P))
-            if k == 2:
-                round_weight("ws11", ws1_bf[:, PACK * PASS :], ws11)
+            if k == ROUND_WS11:
+                round_weight(ws1_bf[:, PACK * PASS :], ws11)
                 both = quantize("ws1", ws1_bf[:])
                 ws_q[1, 0] = both, 0
                 ws_q[1, 1] = both, PASS
-            if k == 4:
-                round_weight("wa1", wa1_bf[:], wa1)
+            if k == ROUND_WA1:
+                round_weight(wa1_bf[:], wa1)
                 wa_q[1] = quantize("wa1", wa1_bf[:])
-            if k == 7:
-                round_wo("wo0", wo_bf[:, : PACK * N], wo0)
-                round_wo("wo1", wo_bf[:, PACK * N :], wo1)
+            if k == ROUND_WO:
+                round_wo(wo_bf[:, : PACK * N], wo0)
+                round_wo(wo_bf[:, PACK * N :], wo1)
                 front = quantize("wo_front", wo_bf[:, : PACK * PASS])
                 back = quantize("wo_back", wo_bf[:, PACK * PASS :])
-                for m in range(GROUPS * OUT_TILES):
-                    wo_q[m] = (front, m * P) if m < PACK else (back, (m - PACK) * P)
+                for w in range(GROUPS * OUT_TILES):
+                    wo_q[w] = (front, w * P) if w < PACK else (back, (w - PACK) * P)
         subtract_and_quantize(*steps[-1])
-        for q in range(15 - STRIPS - 1, STRIPS):
+        for q in range(STRIPS - 2, STRIPS):
             scores(q)

from contextlib import ExitStack

import concourse.mybir as mybir

K, K2, H, N, T, S = 512, 1024, 1024, 384, 4096, 1024
FLOPS = 2 * S * (2 * K * H + K2 * H + H * N)

F32 = mybir.dt.float32
BF16 = mybir.dt.bfloat16
I32 = mybir.dt.int32
U32 = mybir.dt.uint32
U16 = mybir.dt.uint16
U8 = mybir.dt.uint8
FP8X4 = mybir.dt.float8_e4m3fn_x4
FP4X4 = mybir.dt.float4_e2m1fn_x4
ALU = mybir.AluOpType
ACT = mybir.ActivationFunctionType

P = 128
PACK = 4
PASS = P * PACK
RUN = 4
GROUPS = H // PASS
STRIP = 128
STRIPS = S // STRIP
HALF = 512
OUT_TILES = N // P
SIDE_A, SIDE_B = 0, 1

EARLY = HALF // STRIP
E_IN_PSUM = ((0, STRIPS - 3), (0, STRIPS - 2), (0, STRIPS - 1))
RANGES = (((0, 512), (512, 512)), ((0, 512), (512, 256), (768, 128), (896, 128)))
E_AHEAD = 2
ROUND_WS01, ROUND_WS11, ROUND_WA1, ROUND_WO = 1, 2, 4, 7
E_BUFS, DIST_BUFS, SHARED_BANKS = EARLY + E_AHEAD, 3, 4


def tile_list_typewriter_strokes_kernel(
    tc, tab_words, tab_scales, offs, xs_words, xs_scales, wa, wb_words, wb_scales, ws, wo, bo, out
):
    nc = tc.nc
    with ExitStack() as ctx:
        keep = ctx.enter_context(tc.tile_pool(name="keep", bufs=1))
        ring = ctx.enter_context(tc.tile_pool(name="ring", bufs=4))
        psum = ctx.enter_context(tc.psum_pool(name="psum", bufs=2))

        xs_scale = keep.tile([P, S], U8, name="xs_scale", align_bytes=64)
        wb_scale_raw = keep.tile([P, H], U8, name="wb_scale_raw", align_bytes=64)
        tab_scale = keep.tile([P, T], U8, name="tab_scale", align_bytes=64)
        nc.gpsimd.memset(xs_scale[:].bitcast(I32), 0)
        nc.vector.memset(tab_scale[:].bitcast(I32), 0)
        nc.gpsimd.memset(wb_scale_raw[:].bitcast(I32), 0)


        def load_rows(w, a, b):
            raw = ring.tile([P, PACK, PASS], F32, name="raw")
            rows = w[a * PASS : (a + 1) * PASS, b * PASS : (b + 1) * PASS]
            nc.sync.dma_start(out=raw[:], in_=rows.rearrange("(p j) c -> p j c", j=PACK))
            return raw

        def load_wo(b):
            raw = ring.tile([P, PACK, N], F32, name="raw")
            rows = wo.rearrange("(b m t i) n -> b t m i n", b=GROUPS, t=PACK, i=RUN)
            for t in range(PACK):
                nc.sync.dma_start(out=raw[:, t, :], in_=rows[b, t])
            return raw

        def load_xs(half):
            words = keep.tile([P, 2, HALF], I32, name="xs_codes%d" % half, align_bytes=64)
            src = xs_words.rearrange("a p c i -> p a (c i)")
            src = src[:, :, PACK * HALF * half : PACK * HALF * (half + 1)]
            nc.sync.dma_start(out=words[:], in_=src.bitcast(I32))
            return words

        def load_scales(tile, rows):
            for quad in range(4):
                nc.sync.dma_start(
                    out=tile[32 * quad : 32 * quad + 4 * rows.shape[0], :].bitcast(I32),
                    in_=rows[:, 4 * quad : 4 * quad + 4, :].bitcast(I32),
                )


        def round_negated(a, raw):
            grouped = keep.tile([P, PACK * PASS], BF16, name="ws%d0_bf" % a, align_bytes=64)
            src = raw[:].rearrange("p j (m t i) -> p m t i j", t=PACK, i=RUN)
            dst = grouped[:].rearrange("p (t m i j) -> p m t i j", t=PACK, i=RUN, j=PACK)
            cut = dst.shape[1] // 4
            nc.scalar.activation(out=dst[:, :cut], in_=src[:, :cut], func=ACT.Copy, scale=-1.0)
            nc.vector.tensor_scalar(
                out=dst[:, cut:], in0=src[:, cut:], scalar1=-1.0, scalar2=None, op0=ALU.mult
            )
            return grouped

        def copy_in_halves(dst, src):
            cut = dst.shape[1] // 2
            nc.scalar.copy(out=dst[:, :cut], in_=src[:, :cut])
            nc.vector.tensor_copy(out=dst[:, cut:], in_=src[:, cut:])

        def round_weight(grouped, raw):
            src = raw[:].rearrange("p j (m t i) -> p m t j i", t=PACK, i=RUN)
            dst = grouped.rearrange("p (t m i j) -> p m t j i", t=PACK, i=RUN, j=PACK)
            copy_in_halves(dst, src)

        def round_wo(grouped, raw):
            src = raw[:].rearrange("p t (m i) -> p m t i", i=RUN)
            dst = grouped.rearrange("p (m i t) -> p m t i", i=RUN, t=PACK)
            copy_in_halves(dst, src)

        def quantize(name, grouped):
            width = grouped.shape[1] // PACK
            codes = keep.tile([P, width], U32, name=name + "_codes", align_bytes=64)
            scales = keep.tile([P, width], U8, name=name + "_scales", align_bytes=64)
            nc.vector.quantize_mx(out=codes[:].bitcast(FP8X4), scales=scales[:], in_=grouped)
            return codes, scales

        def columns(operand, c0, width):
            codes, scales = operand
            return codes[:, c0 : c0 + width].bitcast(FP8X4), scales[:, c0 : c0 + width]

        def list_half(half):
            return offsets[:, half * HALF // 16 : (half + 1) * HALF // 16]

        def gather_scales(half):
            v_scales[half] = keep.tile([P, HALF], U8, name="v_scales%d" % half, align_bytes=64)
            nc.vector.tensor_copy(v_scales[half][:], tab_scale[:].indirect(list_half(half)))

        def gather_codes(half):
            v_codes[half] = keep.tile([P, HALF], U32, name="v_codes%d" % half, align_bytes=64)
            nc.vector.tensor_copy(v_codes[half][:], tab[:].bitcast(U32).indirect(list_half(half)))


        def woven(bank):
            return bank[:].rearrange("p t n -> p n t")

        def paired(bank):
            return bank[:].rearrange("p t (n i) -> p n t i", i=2)

        def e_passes(bank, b, q, t, start):
            half, c0 = divmod(q * STRIP, HALF)
            for a in range(2):
                operand, w0 = ws_q[b, a]
                lhsT, lhsT_scale = columns(operand, w0 + t * P, P)
                nc.tensor.matmul_mx(
                    out=bank[:, t, :],
                    lhsT=lhsT,
                    lhsT_scale=lhsT_scale,
                    rhs=xs_codes[half][:, a, c0 : c0 + STRIP].bitcast(FP8X4),
                    rhs_scale=xs_scale[4 * a :, q * STRIP : (q + 1) * STRIP],
                    start=start and a == 0,
                    stop=a == 1,
                )

        def strokes(b, q):
            if (b, q) in E_IN_PSUM:
                return
            bank = psum.tile([P, PACK, STRIP], F32, name="bank_e", tag="single", bufs=SHARED_BANKS)
            for t in range(PACK):
                e_passes(bank, b, q, t, True)
            e_sb[b, q] = ring.tile([P, STRIP // 2, PACK, 2], F32, name="e_sb", bufs=E_BUFS)
            nc.scalar.copy(out=e_sb[b, q][:], in_=paired(bank))

        def difference(b, q, side):
            fused = (b, q) in E_IN_PSUM
            half, c0 = divmod(q * STRIP, HALF)
            bank = psum.tile([P, PACK, STRIP], F32, name="bank_%d" % side)
            for t in range(PACK):
                if side == SIDE_A:
                    lhsT, lhsT_scale = columns(wa_q[b], t * P, P)
                else:
                    w0 = b * PASS + t * P
                    lhsT = wb_codes[:, 2 * w0 : 2 * (w0 + P)].bitcast(FP4X4)
                    lhsT_scale = wb_scale[:, w0 : w0 + P]
                nc.tensor.matmul_mx(
                    out=bank[:, t, :],
                    lhsT=lhsT,
                    lhsT_scale=lhsT_scale,
                    rhs=v_codes[half][:, c0 : c0 + STRIP].bitcast(FP8X4),
                    rhs_scale=v_scales[half][:, c0 : c0 + STRIP],
                    start=True,
                    stop=not fused,
                )
                if fused:
                    e_passes(bank, b, q, t, False)
            if (b, q // 2) not in dist:
                dist[b, q // 2] = ring.tile([P, 2, 2, STRIP, PACK], F32, name="dist", bufs=DIST_BUFS)
            if fused:
                nc.scalar.activation(out=dist[b, q // 2][:, q % 2, side], in_=woven(bank), func=ACT.Abs)
                return
            if (b, q) not in diff:
                diff[b, q] = ring.tile([P, 2, STRIP // 2, PACK, 2], F32, name="diff")
            op = ALU.add if b == 0 else ALU.subtract
            nc.vector.tensor_tensor(out=diff[b, q][:, side], in0=paired(bank), in1=e_sb[b, q][:], op=op)

        def absolute(b, q, side0, side1):
            if (b, q) not in E_IN_PSUM:
                nc.scalar.activation(
                    out=dist[b, q // 2][:, q % 2, side0:side1].rearrange("p u (n i) t -> p (u n) i t", i=2),
                    in_=diff[b, q][:, side0:side1].rearrange("p u n t i -> p (u n) i t"),
                    func=ACT.Abs,
                )

        def range_of(b, q):
            return [r for r in RANGES[b] if r[0] <= q * STRIP < r[0] + r[1]][0]

        def subtract_and_quantize(b, q):
            j0, width = range_of(b, q)
            if width > STRIP and q % 2 == 0:
                return
            first = q if width == STRIP else q - 1
            pair = dist[b, q // 2][:, first % 2 : q % 2 + 1].rearrange("p s u n t -> p s u (n t)")
            nc.vector.tensor_tensor(
                out=h_bf[b][:, first * PASS : (q + 1) * PASS].rearrange("p (s c) -> p s c", c=PASS),
                in0=pair[:, :, SIDE_A],
                in1=pair[:, :, SIDE_B],
                op=ALU.subtract,
            )
            if (q + 1) * STRIP == j0 + width:
                h_q[b, j0] = quantize("h%d_%d" % (b, j0), h_bf[b][:, PACK * j0 : PACK * (j0 + width)])

        def scores(q):
            j0, width = range_of(GROUPS - 1, q)
            if (q + 1) * STRIP != j0 + width:
                return
            result = keep.tile([P, OUT_TILES, width], F32, name="result%d" % j0)
            per_bank = min(OUT_TILES, HALF // width)
            for c0 in range(0, OUT_TILES, per_bank):
                tiles = range(c0, min(c0 + per_bank, OUT_TILES))
                bank = psum.tile([P, HALF], F32, name="bank_y", tag="single", bufs=SHARED_BANKS)
                for b in range(GROUPS):
                    h0 = range_of(b, q)[0]
                    rhs, rhs_scale = columns(h_q[b, h0], j0 - h0, width)
                    for c in tiles:
                        lhsT, lhsT_scale = columns(*wo_q[b * OUT_TILES + c], P)
                        nc.tensor.matmul_mx(
                            out=bank[:, (c - c0) * width : (c - c0 + 1) * width],
                            lhsT=lhsT,
                            lhsT_scale=lhsT_scale,
                            rhs=rhs,
                            rhs_scale=rhs_scale,
                            start=b == 0 and c == tiles[0],
                            stop=b == GROUPS - 1 and c == tiles[-1],
                        )
                for c in tiles:
                    nc.scalar.activation(
                        out=result[:, c, :],
                        in_=bank[:, (c - c0) * width : (c - c0 + 1) * width],
                        func=ACT.Tanh,
                        bias=bias[:, c : c + 1],
                    )
            nc.sync.dma_start(out=out[:, j0 : j0 + width].rearrange("(c p) j -> p c j", p=P), in_=result[:])

        xs_codes, v_codes, v_scales = {}, {}, {}
        ws_q, wa_q, wo_q, h_q = {}, {}, {}, {}
        e_sb, diff, dist = {}, {}, {}

        ws00 = load_rows(ws, 0, 0)
        load_scales(xs_scale, xs_scales)
        xs_codes[0] = load_xs(0)
        offsets = keep.tile([P, S // 16], U16, name="offsets")
        nc.sync.dma_start(offsets[:], offs)
        ws10 = load_rows(ws, 1, 0)
        load_scales(tab_scale, tab_scales)
        wb_raw = keep.tile([P, 2 * H], U8, name="wb_raw", align_bytes=64)
        nc.sync.dma_start(out=wb_raw[:].bitcast(I32), in_=wb_words[0].bitcast(I32))
        tab = keep.tile([P, T], I32, name="tab", align_bytes=64)
        nc.sync.dma_start(out=tab[:], in_=tab_words[0].rearrange("p t i -> p (t i)").bitcast(I32))
        load_scales(wb_scale_raw, wb_scales)
        wa0 = load_rows(wa, 0, 0)
        xs_codes[1] = load_xs(1)
        ws01 = load_rows(ws, 0, 1)

        for a, raw in enumerate((ws00, ws10)):
            ws_q[0, a] = quantize("ws%d0" % a, round_negated(a, raw)[:]), 0
        ws11 = load_rows(ws, 1, 1)
        wa1 = load_rows(wa, 0, 1)
        for q in range(EARLY):
            strokes(0, q)
        gather_scales(0)
        wb_codes = keep.tile([P, 2 * H], U8, name="wb_codes", align_bytes=64)
        wb_scale = keep.tile([P, H], U8, name="wb_scale", align_bytes=64)
        for dst, src, words in ((wb_codes, wb_raw, 2), (wb_scale, wb_scale_raw, 1)):
            nc.vector.tensor_copy(
                out=dst[:].bitcast(I32).rearrange("p (b t m w) -> p b t m w", b=GROUPS, t=PACK, w=words),
                in_=src[:].bitcast(I32).rearrange("p (b m t w) -> p b t m w", b=GROUPS, t=PACK, w=words),
            )
        gather_scales(1)
        gather_codes(0)
        wa0_bf = keep.tile([P, PACK * PASS], BF16, name="wa0_bf", align_bytes=64)
        round_weight(wa0_bf[:], wa0)
        wa_q[0] = quantize("wa0", wa0_bf[:])
        wo0 = load_wo(0)
        for q in range(EARLY):
            difference(0, q, SIDE_B)
            absolute(0, q, SIDE_B, SIDE_B + 1)
        gather_codes(1)

        h_bf = [keep.tile([P, PACK * S], BF16, name="h_bf%d" % b, align_bytes=64) for b in range(GROUPS)]
        ws1_bf = keep.tile([P, 2 * PACK * PASS], BF16, name="ws1_bf", align_bytes=64)
        wa1_bf = keep.tile([P, PACK * PASS], BF16, name="wa1_bf", align_bytes=64)
        wo_bf = keep.tile([P, GROUPS * PACK * N], BF16, name="wo_bf", align_bytes=64)

        steps = [(b, q) for b in range(GROUPS) for q in range(STRIPS)]
        for k, (b, q) in enumerate(steps):
            if EARLY <= k + E_AHEAD < len(steps):
                strokes(*steps[k + E_AHEAD])
            difference(b, q, SIDE_A)
            if k < EARLY:
                absolute(b, q, SIDE_A, SIDE_A + 1)
            else:
                difference(b, q, SIDE_B)
                absolute(b, q, SIDE_A, SIDE_B + 1)
            if k > 0:
                subtract_and_quantize(*steps[k - 1])
            if STRIPS < k < len(steps) - 1:
                scores(q - 1)
            if k == ROUND_WS01:
                round_weight(ws1_bf[:, : PACK * PASS], ws01)
                wo1 = load_wo(1)
                bias = keep.tile([P, OUT_TILES], F32, name="bias")
                with nc.allow_non_contiguous_dma(reason="one bias value a partition"):
                    nc.sync.dma_start(out=bias[:], in_=bo.rearrange("(c p) -> p c", p=P))
            if k == ROUND_WS11:
                round_weight(ws1_bf[:, PACK * PASS :], ws11)
                both = quantize("ws1", ws1_bf[:])
                ws_q[1, 0] = both, 0
                ws_q[1, 1] = both, PASS
            if k == ROUND_WA1:
                round_weight(wa1_bf[:], wa1)
                wa_q[1] = quantize("wa1", wa1_bf[:])
            if k == ROUND_WO:
                round_wo(wo_bf[:, : PACK * N], wo0)
                round_wo(wo_bf[:, PACK * N :], wo1)
                front = quantize("wo_front", wo_bf[:, : PACK * PASS])
                back = quantize("wo_back", wo_bf[:, PACK * PASS :])
                for w in range(GROUPS * OUT_TILES):
                    wo_q[w] = (front, w * P) if w < PACK else (back, (w - PACK) * P)
        subtract_and_quantize(*steps[-1])
        for q in range(STRIPS - 2, STRIPS):
            scores(q)
